import numpy as np, ml_dtypes
CORES = [35,38,43,46]
N = 4
BF = ml_dtypes.bfloat16
def gentries(a):
    return np.ascontiguousarray(a.reshape(8, 16, -1).transpose(0, 2, 1)).reshape(8, -1)
def gtable(e):
    e = np.asarray(e); return np.ascontiguousarray(e.reshape(8, -1, 16).transpose(0, 2, 1)).reshape(128, -1).astype(np.int32)
V, S, L, DS = 4096, 128, 16, (1, 2, 3)
W = N * V
def mix(rng, a):
    return np.take_along_axis(a, np.argsort(rng.random(a.shape), axis=-1), -1)
def some(rng, pool, shape, n):
    q = len(pool) // n
    return pool[np.arange(n) * q + rng.integers(0, q, shape + (n,))]
def parts(rng):
    x = (256 * np.sqrt(rng.random((N, 8, 1, V))) * rng.random((N, 8, 16, V))).astype(np.int64)
    sl = np.empty((N, 8, S, L), np.int64)
    for g in range(8):
        p = rng.permutation(W); a = p[:3 * L][np.argsort(rng.random((N, S, 3 * L)), axis=-1)[..., :L]]
        sl[:, g] = np.where(np.arange(L) < rng.integers(0, L + 1, (N, S, 1)), a, some(rng, p[3 * L:], (N, S), L))
    return x, mix(rng, sl), rng.integers(0, S * L, (N, 8, V))
def pack(x, sl, pr):
    return {"x": np.ascontiguousarray(x.reshape(N, 128, V)).astype(np.float32).astype(BF), "sl": np.stack([gtable(a.reshape(8, -1)) for a in sl]), "prey": np.stack([gtable(a) for a in pr])}
def setup_inputs(rng):
    return pack(*parts(rng))
def setup_inputs_pools(rng):
    x, sl, pr = parts(rng)
    for g in range(8):
        x[:, g] = rng.integers(0, 256, 16)[np.argsort(rng.random((N, 16, V)), axis=1)]
    ms = np.array([0, 1, 2, L // 2, L - 1, L])
    for a in range(N):
        b = a ^ DS[0]
        if a < b:
            for g in range(8):
                e = some(rng, rng.permutation(W), (S,), 2 * L); m = rng.choice(ms, (S, 1)); m[:6, 0] = ms
                if g == 2: m[:] = 0
                if g == 5: m[:] = L
                sl[a, g] = mix(rng, e[:, :L]); sl[b, g] = mix(rng, np.where(np.arange(L) < m, e[:, L:], e[:, :L]))
    return pack(x, sl, pr)
def setup_inputs_ties(rng):
    x, sl, pr = parts(rng)
    kind = rng.integers(0, 4, (N, 8, V)); proto = rng.integers(0, 256, (8, 16, 4))
    proto[1, :, 1] = proto[1, ::-1, 0]; proto[1, :, 3] = proto[1, ::-1, 2]; proto[0] = rng.integers(0, 256, (1, 1))
    for q in range(N):
        for g in range(8): x[q, g] = proto[g][:, kind[q, g]]
    return pack(x, sl, pr)
def setup_inputs_few(rng):
    x, sl, pr = parts(rng); o = rng.permutation(N)
    for g in (0, 4):
        c = np.concatenate([np.array([0, W - 1]), 1 + rng.permutation(W - 2)[:L]])
        sl[:, g] = c[np.argsort(rng.random((N, S, L + 2)), axis=-1)[..., :L]]
    pr[:, 1] = rng.choice(np.array([0, L - 1, L, S * L - 1]), (N, V)); pr[:, 5] = S * L - 1
    sl[1:, 5] = sl[0, 5]
    sl[:, 2] = mix(rng, some(rng, o[0] * V + rng.permutation(V), (N, S), L))
    sl[:, 6] = mix(rng, some(rng, o[1] * V + 1024 * rng.integers(0, V // 1024) + rng.permutation(1024), (N, S), L))
    for g in (3, 7): sl[:, g] = mix(rng, np.zeros((N, S, 1), np.int64) + rng.permutation(W)[:L])
    return pack(x, sl, pr)
def setup_inputs_ends(rng):
    x, sl, pr = parts(rng); x = 255 * rng.integers(0, 2, x.shape)
    for g in (0, 3, 6): x[:, g, :, 0::2] = 0; x[:, g, :, 1::2] = 255
    x[:, 1, :, 0::2] = rng.integers(0, 32, (N, 16, V // 2)); x[:, 1, :, 1::2] = rng.integers(224, 256, (N, 16, V // 2))
    c = np.arange(V); low = 255 * (L - 1) // (2 * L - 1); e = rng.integers(0, 4, (N, 16, V))
    x[:, 2] = np.where(np.arange(16)[:, None] % L == (c // 2) % L, 255 * (1 - c % 2), np.where(c % 2 == 1, 255 - low + e, low - e))
    for a in range(N):
        odd = int(a > (a ^ DS[0]))
        sl[a, 0] = some(rng, 2 * rng.permutation(W // 2) + odd, (S,), L); sl[a, 3] = some(rng, 2 * rng.permutation(W // 2) + 1 - odd, (S,), L)
        sl[a, 1] = some(rng, 2 * rng.permutation(W // 2) + odd, (S,), L)
        sl[a, 2] = mix(rng, 2 * (L * rng.integers(0, W // (2 * L), (S, L)) + np.arange(L)) + odd)
    t = np.arange(S)
    for a in range(N):
        b = a ^ DS[0]
        if a < b: sl[b, 0, t, rng.integers(0, L, S)] = sl[a, 0, t, rng.integers(0, L, S)]
    sl[:, 4] = np.concatenate([rng.permutation(W) for i in range((N * S * L + W - 1) // W)])[:N * S * L].reshape(N, S, L)
    one = rng.integers(0, N) * V + np.concatenate([rng.permutation(V) for i in range((S * L + V - 1) // V)])[:S * L].reshape(S, L)
    sl[:, 5] = mix(rng, np.zeros((N, 1, 1), np.int64) + one)
    sl[:, 7] = mix(rng, some(rng, 16 * rng.permutation(W // 16) + rng.integers(0, 16), (N, S), L))
    for g in (4, 5): pr[:, g] = mix(rng, np.zeros((N, 1), np.int64) + np.arange(max(V, S * L)) % (S * L))[:, :V]
    return pack(x, sl, pr)
def setup_inputs_spread(rng):
    x, sl, pr = parts(rng)
    x = (np.exp2(8 * rng.random((N, 8, 1, V))) * rng.random((N, 8, 16, V)) * (rng.random((N, 8, 1, V)) > 0.0625)).astype(np.int64)
    pr = np.minimum((S * L * rng.random((N, 8, V)) ** 3).astype(np.int64), S * L - 1)
    return pack(x, sl, pr)
def check_inputs(d):
    bad = []
    v = np.asarray(d["x"]).astype(np.float32)
    if not np.all((v >= 0) & (v <= 255) & (v == np.floor(v))): bad.append("range of x")
    for k, hi in (("sl", W - 1), ("prey", S * L - 1)):
        if np.min(d[k]) < 0 or np.max(d[k]) > hi: bad.append("range of " + k)
    e = np.sort(np.stack([gentries(a) for a in d["sl"]]).reshape(N, 8, S, L), axis=-1)
    if np.any(e[..., 1:] == e[..., :-1]): bad.append("different species in a site of sl")
    return bad
def reference(x, sl, prey):
    v = x.astype(np.float32).astype(np.int64).reshape(N, 8, 16, V)
    ls = np.stack([gentries(a) for a in sl]).astype(np.int64).reshape(N, 8, S, L); pl = np.stack([gentries(a) for a in prey]).astype(np.int64)
    j = np.arange(L)
    for d in DS:
        w = np.concatenate([v[a] for a in range(N)], axis=2)
        cs, od = [], []
        for a in range(N):
            c = np.add.reduce(np.take_along_axis(w, ls[a].reshape(8, 1, S * L), 2).reshape(8, 16, S, L), axis=3)
            cs.append(c); od.append(np.argsort(np.arange(S) - S * np.add.reduce(c, axis=1), axis=1))
        new = np.array(ls)
        for a in range(N):
            b = a ^ d
            if a < b:
                la = np.take_along_axis(ls[a], od[a][:, :, None], 1); lb = np.take_along_axis(ls[b], od[b][:, :, None], 1)
                ca = np.take_along_axis(cs[a], od[a][:, None, :], 2)[..., None]; cb = np.take_along_axis(cs[b], od[b][:, None, :], 2)[..., None]
                pool = np.concatenate([la, lb], axis=2)
                px = L * np.take_along_axis(w, pool.reshape(8, 1, -1), 2).reshape(8, 16, S, 2 * L)
                key = 2 * L * np.add.reduce(np.abs(px - ca) - np.abs(px - cb), axis=1) + np.arange(2 * L)
                eq = la[:, :, :, None] == lb[:, :, None, :]
                com = np.concatenate([np.any(eq, axis=3), np.any(eq, axis=2)], axis=2)
                m = np.add.reduce((~com[:, :, :L]).astype(np.int64), axis=2)[:, :, None]
                sp = np.take_along_axis(pool, np.argsort(np.where(com, 2 ** 40 + np.arange(2 * L), key), axis=2), 2)
                np.put_along_axis(new[a], od[a][:, :, None], np.take_along_axis(sp, np.where(j < m, j, m + j), 2), 1)
                np.put_along_axis(new[b], od[b][:, :, None], np.take_along_axis(sp, np.where(j < m, m + j, L + j), 2), 1)
        ls = new
        hx = [np.take_along_axis(w, np.take_along_axis(ls[a].reshape(8, S * L), pl[a], 1)[:, None, :], 2) for a in range(N)]
        v = (v + np.stack(hx) + 1) >> 1
    return {"yl": np.stack([gtable(a.reshape(8, -1)) for a in ls]).astype(np.float32), "yx": v.reshape(N, 128, V).astype(np.float32)}

@@ -1,0 +1,558 @@
+from concourse.bass import DstId, RemoteDMATransfer
+from concourse.mybir import AluOpType, ActivationFunctionType
+
+BF, FH, FF, I4, U2 = "bfloat16", "float16", "float32", "int32", "uint16"
+S6 = [128, 8, 2, 2, 2, 2]
+_SB = {
+    "SL": ([128, 128], I4), "PR": ([128, 256], I4), "XW": ([128, 4128], BF),
+    "LISTS": ([128, 512], U2), "OFF": ([128, 512], U2), "REP": ([128, 6144], BF),
+    "PREYL": ([128, 256], U2), "ILST": ([128, 128], U2),
+    "q0": ([128, 128], I4), "q1": ([128, 128], I4), "q2": ([128, 128], I4),
+    "w0": ([128, 256], I4), "w1": ([128, 256], I4), "w2": ([128, 256], I4), "w3": ([128, 256], I4), "w4": ([128, 256], I4),
+    "PT": ([128, 2048], BF), "IDT": ([128, 1280], BF), "PWIN": ([128, 16384], BF),
+    "ALLT0": ([128, 8192], BF), "ALLT1": ([128, 8192], BF), "POOL": ([128, 4096], BF),
+    "INF0": ([128, 4096], BF), "INF1": ([128, 4096], BF), "INF2": ([128, 4096], BF), "INF3": ([128, 2048], BF),
+    "V": ([128, 4096], BF), "VS": ([128, 2048], FH), "VT": ([128, 2048], FH), "VM": ([128, 1024], FF), "HALF": ([128, 512], BF),
+    "YXO": ([128, 4096], FF), "SU": ([128, 1024], FH), "V16": ([128, 2048], FH),
+    "E1O": ([128, 256], FH), "E1P": ([128, 768], FH), "CW": ([128, 128], FF), "CPW": ([128, 128], FF),
+    "G": ([128, 1024], BF), "MA": ([128, 1024], BF), "MAF": ([128, 1024], FF), "MLL": ([128, 128], U2), "TPX": ([128, 128], FF),
+    "IDSO": ([128, 256], BF), "IDSP": ([128, 768], BF), "IDO": ([128, 16, 16], FF), "PAF": ([128, 128], FF), "PAL": ([128, 128], U2),
+    "Y1": ([128, 2048], FH), "Y2": ([128, 2048], FH), "EQ": ([128, 2048], BF),
+    "NC": ([128, 128], FF), "CB": ([128, 128], FF), "K1": ([128, 128], FF),
+    "SRA": (S6, FF), "SRB": (S6, FF), "SRM": (S6, FF), "E2O": ([128, 128], FF), "E2P": ([128, 384], FF),
+    "SI": ([128, 128], I4), "QA": ([128, 128], I4), "BB": ([128, 128], I4), "M1": ([128, 128], FF), "A1": ([128, 128], FF),
+    "DIF": ([128, 128], FF), "ADJ": ([128, 128], FF), "LST": ([128, 128], U2), "YLO": ([128, 128], FF),
+    "ONE": ([128, 128], BF), "IB": ([128, 128], BF), "IF": ([128, 128], FF), "TC": ([128, 1024], BF),
+    "B8a": ([128, 8], BF), "B8": ([128, 8], BF), "BE": ([128, 1024], BF), "NBE": ([128, 1024], BF),
+    "GS": ([128, 1024], BF), "TS": ([128, 1024], BF), "PC": ([128, 1], FF), "PCI": ([128, 1], I4), "P16I": ([128, 1], I4),
+    "P16": ([128, 1], FF), "CD": ([128, 1], FF), "CE": ([128, 1], FF), "T16": ([128, 128], FF), "TC16": ([128, 16], BF),
+    "QC": ([128, 128], BF), "QC2": ([128, 128], BF), "QB": ([128, 128], FF), "QB2": ([128, 128], FF),
+    "BP": ([128, 8], FH), "BN": ([128, 8], FH), "BXP": ([128, 128], BF), "BXN": ([128, 128], BF),
+    "WC": ([128, 8], FF), "SEL": ([128, 32], BF), "CLI": ([128, 128], I4), "CL": ([128, 128], U2), "N16": ([128, 256], I4),
+}
+SCRATCH = {k: ("sbuf", s, d) for k, (s, d) in _SB.items()}
+_PS = {"PS%d" % i: ([128, 16, 32] if i == 5 else [128, 512], FF) for i in range(8)}
+for _k, (_s, _d) in _PS.items():
+    SCRATCH[_k] = ("psum", _s, _d)
+SEMAPHORES = (["cv", "cs", "ct", "cg", "dsl", "dpr", "dx0", "dx1", "dpw0", "dpw1", "dyl"] + ["dyx%d" % i for i in range(4)]
+              + ["ali%d" % i for i in range(4)] + ["arep%d" % i for i in range(4)]
+              + ["apt", "lli", "lpt", "lrep", "linf", "lids", "lst", "le1", "le2", "le3"]
+              + [n + str(k) for n in ("ainf", "aids", "ast", "ae1", "ae2", "ae3") for k in range(3)])
+
+ADD, MUL, MAX, MIN = AluOpType.add, AluOpType.mult, AluOpType.max, AluOpType.min
+GT, GE, LT, EQU = AluOpType.is_gt, AluOpType.is_ge, AluOpType.is_lt, AluOpType.is_equal
+SHR, AND = AluOpType.arith_shift_right, AluOpType.bitwise_and
+COPY = ActivationFunctionType.Copy
+ALL = slice(None)
+BIG = 4194304.0
+MAGIC = 12582912.0
+DS = (1, 2, 3)
+
+
+def rank_program(g, core, T, topo):
+    me = T.rank_of(core)
+    if me is None:
+        return
+    cores = list(T.cores)
+    nrank = len(cores)
+    Q = {"v": g.vector, "s": g.scalar, "t": g.tensor, "g": g, "y": g.sync}
+    know = {q: {} for q in Q}
+    tot = {}
+    log = {}
+
+    def V(name, *idx, ps=ALL, tag=None):
+        shape = SCRATCH[name][1][1:]
+        st = [1] * len(shape)
+        for i in range(len(shape) - 2, -1, -1):
+            st[i] = st[i + 1] * shape[i + 1]
+        full = list(idx) + [ALL] * (len(shape) - len(idx))
+        m = 1
+        for x, n, w in reversed(list(zip(full, shape, st))):
+            r = range(x, x + 1) if isinstance(x, int) else range(*x.indices(n))
+            if m == (1 << w) - 1 and r.step == 1:
+                m = ((1 << (w * len(r))) - 1) << (w * r[0])
+            else:
+                m = sum(m << (i * w) for i in r)
+        return {"ap": T[name][tuple([ps] + full)], "n": name, "m": m, "tag": tag}
+
+    def C(name, a, b, step=1, **kw):
+        return V(name, slice(a, b, step), **kw)
+
+    def need(q, evs):
+        for sem, cnt, sn in sorted(evs, key=lambda e: -len(e[2])):
+            if know[q].get(sem, 0) >= cnt:
+                continue
+            c = tot[sem] if sem[0] in "dl" else cnt
+            Q[q].wait_ge(T.sem[sem], c)
+            k = know[q]
+            for s_, c_ in list(sn.items()) + [(sem, c)]:
+                if k.get(s_, 0) < c_:
+                    k[s_] = c_
+
+    def touch(q, ins, outs):
+        evs = []
+        for kind, lst in (("r", ins), ("w", outs)):
+            for r in lst:
+                if r["n"] in _PS:
+                    d = log.setdefault(r["n"], {})
+                    for oq in list(d):
+                        if oq != q:
+                            evs.append(d[oq])
+                            del d[oq]
+                    continue
+                for e in log.get(r["n"], ()):
+                    if not e[0] & r["m"] or (kind == "r" and e[2] == "r"):
+                        continue
+                    if e[1] is not None and r["tag"] is not None and e[1] != r["tag"]:
+                        continue
+                    evs.append(e[3])
+        return evs
+
+    def note(q, ins, outs, ev):
+        for kind, lst in (("r", ins), ("w", outs)):
+            for r in lst:
+                if r["n"] in _PS:
+                    log.setdefault(r["n"], {})[q] = ev
+                    continue
+                old = log.get(r["n"], [])
+                if kind == "w":
+                    old = [e for e in old if e[0] & ~r["m"] or (r["tag"] is not None and r["tag"] != e[1])]
+                log[r["n"]] = old + [(r["m"], r["tag"], kind, ev)]
+
+    def done(q, sem, n):
+        tot[sem] = tot.get(sem, 0) + n
+        d = dict(know[q])
+        d[sem] = tot[sem]
+        return (sem, tot[sem], d)
+
+    def op(q, fn, ins, outs):
+        need(q, touch(q, ins, outs))
+        ev = done(q, "c" + q, 1)
+        fn().then_inc(T.sem["c" + q], 1)
+        note(q, ins, outs, ev)
+
+    def dma(q, sem, out, in_, ext_out=None, ext_in=None):
+        ins, outs = [in_] if in_ else [], [out] if out else []
+        need(q, touch(q, ins, outs))
+        ev = done(q, sem, 16)
+        Q[q].dma_start(out["ap"] if out else ext_out, in_["ap"] if in_ else ext_in).then_inc(T.sem[sem], 16)
+        note(q, ins, outs, ev)
+
+    def expect(sem, cnt, outs):
+        tot[sem] = tot.get(sem, 0) + cnt
+        note("net", [], outs, (sem, tot[sem], {sem: tot[sem]}))
+
+    others = [r for r in range(nrank) if r != me]
+    off = [r for r in others if topo.chip(cores[r]) != topo.chip(core)]
+    on = [r for r in others if r not in off]
+    e_off = list(topo.engines(core, cores[off[0]]))
+    e_on = [e for e in topo.engines(core, cores[on[0]]) if e not in e_off]
+    NB = len(e_off)
+
+    def did(r):
+        rid, pid, _ = topo.addr(cores[r])
+        return DstId(rid=rid, pnc=pid)
+
+    def ecount(src):
+        return len(topo.engines(cores[src], core))
+
+    def send(r, sem, lsem, dst, src):
+        need("g", touch("g", [src], []))
+        rid, pid, _ = topo.addr(cores[r])
+        ev = done("g", lsem, len(topo.engines(core, cores[r])))
+        g.remote_dma(dst["ap"], src["ap"], T.sem[sem], T.sem[lsem], pid, rid, topo.mask(core, cores[r]))
+        note("g", [src], [], ev)
+
+    def send_all(sem, lsem, x):
+        need("g", touch("g", [x], []))
+        tr = [RemoteDMATransfer(dst_ids=[did(r) for r in rs], dma_engine_mask=sum(1 << e for e in es), remote_sem=T.sem[sem],
+                                srcs=[x["ap"]], dsts=[x["ap"] for r in rs], alu_op=0) for rs, es in ((off, e_off), (on, e_on))]
+        ev = done("g", lsem, len(e_off) + len(e_on))
+        g.remote_dma_fused(tr, local_sem=T.sem[lsem])
+        note("g", [x], [], ev)
+
+    def ts(out, a, s1, s2, op0, op1=None):
+        ins = [a] + [s for s in (s1, s2) if isinstance(s, dict)]
+        x1 = s1["ap"] if isinstance(s1, dict) else s1
+        x2 = s2["ap"] if isinstance(s2, dict) else s2
+        if op1 is None:
+            op("v", lambda: g.vector.tensor_scalar(out["ap"], a["ap"], x1, None, op0), ins, [out])
+        else:
+            op("v", lambda: g.vector.tensor_scalar(out["ap"], a["ap"], x1, x2, op0, op1), ins, [out])
+
+    def tt(out, a, b, o):
+        op("v", lambda: g.vector.tensor_tensor(out["ap"], a["ap"], b["ap"], o), [a, b], [out])
+
+    def ttg(out, win, lst, b, o):
+        op("v", lambda: g.vector.tensor_tensor(out["ap"], win["ap"].indirect(lst["ap"]), b["ap"], o), [win, lst, b], [out])
+
+    def vcopy(out, a):
+        op("v", lambda: g.vector.tensor_copy(out["ap"], a["ap"]), [a], [out])
+
+    def vgather(out, win, lst):
+        op("v", lambda: g.vector.tensor_copy(out["ap"], win["ap"].indirect(lst["ap"])), [win, lst], [out])
+
+    def sgather(out, win, lst):
+        op("s", lambda: g.scalar.activation(out["ap"], win["ap"].indirect(lst["ap"]), COPY), [win, lst], [out])
+
+    def scopy(out, a, bias=0.0, scale=1.0):
+        op("s", lambda: g.scalar.activation(out["ap"], a["ap"], COPY, bias=bias, scale=scale), [a], [out])
+
+    def fill(out, c):
+        op("v", lambda: g.vector.memset(out["ap"], c), [], [out])
+
+    def mm(out, l, r, start, stop):
+        op("t", lambda: g.tensor.matmul(out["ap"], l["ap"], r["ap"], start, stop), [l, r], [out])
+
+    def iota(out, pattern, cm, small=True):
+        if small:
+            op("g", lambda: g.iota(out["ap"], pattern, 0, cm, allow_small_or_imprecise_dtypes=True), [], [out])
+        else:
+            op("g", lambda: g.iota(out["ap"], pattern, 0, cm), [], [out])
+
+    def afs(out, a, pattern, cmp, base, cm):
+        op("g", lambda: g.affine_select(out["ap"], a["ap"], pattern, cmp, 0.0, base, cm), [a], [out])
+
+    def blk(name, r):
+        return C(name, 2048 * r, 2048 * r + 2048)
+
+    def row(name, i, n=128):
+        return C(name, n * i, n * i + n)
+
+    dma("y", "dsl", V("SL"), None, ext_in=T.sl[:, :])
+    dma("s", "dpr", V("PR"), None, ext_in=T.prey[:, :])
+    dma("y", "dx0", C("XW", 16, 2064), None, ext_in=T.x[:, 0:2048])
+    dma("s", "dx1", C("XW", 2064, 4112), None, ext_in=T.x[:, 2048:4096])
+    fill(V("ONE"), 1.0)
+    fill(C("XW", 0, 16), 0.0)
+    fill(C("XW", 4112, 4128), 0.0)
+    iota(V("PC"), [[0, 1]], 1)
+    iota(V("PCI"), [[0, 1]], 1, False)
+    afs(V("B8a"), C("ONE", 0, 8), [[-16, 8]], GE, 0, 1)
+    afs(V("B8"), V("B8a"), [[16, 8]], GE, 15, -1)
+    afs(V("IB"), V("ONE"), [[-1, 128]], EQU, 0, 1)
+    iota(V("N16"), [[16, 256]], 0, False)
+    vcopy(row("LISTS", me), V("SL"))
+    send_all("ali%d" % me, "lli", row("LISTS", me))
+
+    def offsets(q):
+        ts(row("OFF", q), row("LISTS", q), 16.0 - 4096.0 * me, 4112.0, ADD, MIN)
+    offsets(me)
+    vcopy(V("PREYL"), V("PR"))
+    ts(V("w0"), V("PR"), 2048 * me, None, ADD)
+    ts(V("w1"), V("w0"), 7, None, SHR)
+    ts(V("w2"), V("w0"), 127, None, AND)
+    vcopy(C("PT", 512 * me, 512 * me + 256), V("w1"))
+    vcopy(C("PT", 512 * me + 256, 512 * me + 512), V("w2"))
+    send_all("apt", "lpt", row("PT", me, 512))
+    iota(V("CLI"), [[1, 128]], 0, False)
+    iota(V("QC"), [[0, 8], [1, 16]], 0)
+    iota(V("TC16"), [[0, 16]], 1)
+    iota(V("T16"), [[0, 128]], 16)
+    fill(C("PWIN", 0, 4096), 0.0)
+    for r in others:
+        expect("ali%d" % r, NB, [row("LISTS", r)])
+    expect("apt", NB * (nrank - 1), [row("PT", r, 512) for r in others])
+    scopy(C("PWIN", 4096, 8192), C("PWIN", 0, 4096))
+    ts(V("P16I"), V("PCI"), 15, None, AND)
+    vcopy(V("P16"), V("P16I"))
+    ts(V("w3"), V("N16"), V("P16"), None, ADD)
+    ts(V("w4"), V("w3"), 127, None, AND)
+    vcopy(C("IDT", 1024, 1280), V("w4"))
+    ts(V("w4"), V("w3"), 7, None, SHR)
+    for o in range(nrank):
+        ts(row("IDT", o, 256), V("w4"), 32 * o, None, ADD)
+    order = [off[me % 2], off[1 - me % 2], on[0]]
+    for q in order:
+        offsets(q)
+    for i, q in enumerate(order):
+        (sgather if i != 1 else vgather)(row("REP", i, 2048), V("XW"), row("OFF", q))
+    for i in range(3):
+        send(order[i], "arep%d" % me, "lrep", blk("ALLT0", me), row("REP", i, 2048))
+    for r in others:
+        expect("arep%d" % r, ecount(r), [blk("ALLT0", r)])
+    vgather(blk("ALLT0", me), V("XW"), row("OFF", me))
+    iota(V("TC"), [[0, 8], [1, 128]], -1)
+    fill(C("PWIN", 8192, 12288), 0.0)
+    fill(C("PWIN", 12288, 16384), 0.0)
+
+    for c in range(4):
+        for o in range(nrank):
+            src = row("IDT", o if c == 0 else 4, 256) if c < 2 else row("PT", 2 * o + c - 2, 256)
+            dma("y", "dpw%d" % (c // 2), C("PWIN", 4096 * o, 4096 * o + 4096, ps=slice(c, 128, 16), tag=c), src)
+    ts(V("q0"), V("SL"), 4, None, SHR)
+    ts(V("q1"), V("SL"), 15, None, AND)
+    ts(V("q2"), V("SL"), 12, None, SHR)
+    ts(V("q1"), V("q1"), 256, None, MUL)
+    ts(V("q2"), V("q2"), 3840, None, MUL)
+    tt(V("q0"), V("q0"), V("q1"), ADD)
+    tt(V("q0"), V("q0"), V("q2"), ADD)
+    vcopy(V("ILST"), V("q0"))
+
+    for c, (e, w) in enumerate(((0.0, 128.0), (1.0, 1.0), (2.0, 128.0), (3.0, 1.0))):
+        ts(C("WC", c, c + 1), V("P16"), e, w, EQU, MUL)
+    tt(C("WC", 4, 5), C("WC", 0, 1), C("WC", 1, 2), ADD)
+    tt(C("WC", 5, 6), C("WC", 2, 3), C("WC", 3, 4), ADD)
+    for c, w in enumerate((0, 1, 4, 5)):
+        ts(row("SEL", c, 8), V("B8"), C("WC", w, w + 1), None, MUL)
+    for i in range(8):
+        ts(row("BE", i), V("ONE"), C("B8", i, i + 1), 128.0, MUL, MUL)
+    ts(V("NBE"), V("BE"), -1.0, None, MUL)
+    fill(V("GS"), 0.0)
+    for i in range(8):
+        fill(C("GS", 144 * i, 144 * i + 16), 1.0)
+    vcopy(V("CL"), V("CLI"))
+    fill(V("HALF"), 0.5)
+    for i in range(8):
+        ts(row("BXP", i, 16), C("ONE", 0, 16), C("B8", i, i + 1), 32.0, MUL, MUL)
+    ts(V("BXN"), V("BXP"), -1.0, None, MUL)
+    ts(V("BP"), V("B8"), 1024.0, None, MUL)
+    ts(V("BN"), V("B8"), -1024.0, None, MUL)
+    vcopy(V("IF"), V("IB"))
+    ts(V("QC2"), V("QC"), 16.0, None, ADD)
+
+    inf = ["INF0", "INF1", "INF2", "INF3"]
+
+    def info_done(k, nxt):
+        for j in range(16):
+            mm(C("PS4", j, 512, 16), C(inf[k], j, 2048, 16), V("SEL"), True, True)
+        if nxt is not None:
+            scopy(V("IDSO"), C("PS4", 0, 256))
+            send(me ^ nxt, "aids%d" % k, "lids", row("IDSP", k, 256), V("IDSO"))
+        if nxt is not None and k > 0:
+            scopy(V("PAF"), C("PS4", 384, 512))
+            mm(C("PS7", 0, 128), V("PAF"), V("IF"), True, True)
+            vcopy(V("PAL"), C("PS7", 0, 128))
+        scopy(V("IDO", slice(0, 8)), C("PS4", 256, 384))
+        if nxt is not None:
+            scopy(V("IDO", slice(8, 16)), C("PS4", 256, 384))
+
+    sgather(C("INF0", 0, 2048), V("PWIN"), V("ILST"))
+    banks = ("PS0", "PS1", "PS6", "PS7")
+    for n, r in enumerate([me] + on + off):
+        if n == 3:
+            info_done(0, DS[0])
+        for i, b in enumerate(banks):
+            mm(V(b), V("IB"), row("ALLT0", 4 * r + i, 512), n == 0, n == 3)
+    for i, b in enumerate(banks):
+        if i % 2 == 0:
+            ts(row("POOL", i, 512), V(b), -128.0, None, ADD)
+        else:
+            scopy(row("POOL", i, 512), V(b), bias=-128.0)
+    scopy(V("V"), C("XW", 16, 4112), bias=-128.0)
+
+    def vgath(a, b, tab):
+        sgather(C("REP", a, b), blk(tab, me), C("PREYL", a // 16, b // 16))
+
+    def vsum(a, bank):
+        mm(V(bank), V("IB"), V("HALF"), True, False)
+        mm(V(bank), V("IB"), C("V", a, a + 512), False, False)
+        mm(V(bank), V("IB"), C("REP", a, a + 512), False, True)
+
+    def vround(a, bank, out=None, add=0.0):
+        m = C("VM", a % 1024, a % 1024 + 512)
+        scopy(m, V(bank), scale=0.5, bias=MAGIC)
+        scopy(C("V", a, a + 512) if out is None else out, m, bias=add - MAGIC)
+
+    def vdve(a, b, tab):
+        ttg(C("VS", a, b), blk(tab, me), C("PREYL", a // 16, b // 16), C("V", a, b), ADD)
+        ts(C("VT", a, b), C("VS", a, b), 0.5, 1536.25, MUL, ADD)
+        ts(C("YXO", a, b), C("VT", a, b), -1408.0, None, ADD)
+
+    bits = {1: 5, 2: 4, 4: 3, 8: 2}
+
+    def half(name, s, sv, k=None, kv=None):
+        ix = [ALL] * 6
+        ix[bits[s]] = sv
+        if k is not None:
+            ix[bits[k]] = kv
+        return V(name, *ix[1:])
+
+    def stage(src, dst, s, k=None, desc=False):
+        for kv in ((0, 1) if k else (None,)):
+            lo, hi = half(src, s, 0, k, kv), half(src, s, 1, k, kv)
+            if dst in ("E2O", "SI"):
+                dl, dh = C(dst, 0, 128, 2), C(dst, 1, 128, 2)
+            else:
+                dl, dh = half(dst, s, 0, k, kv), half(dst, s, 1, k, kv)
+            if desc != (kv == 1):
+                dl, dh = dh, dl
+            tt(dl, lo, hi, MIN)
+            tt(dh, lo, hi, MAX)
+
+    def merge(src, other, last, desc=False):
+        stage(src, other, 8, None, desc)
+        stage(other, src, 4, None, desc)
+        stage(src, other, 2, None, desc)
+        stage(other, last, 1, None, desc)
+
+    prev = None
+    for k, d in enumerate(DS):
+        p = me ^ d
+        isA = me < p
+        npart = ecount(p)
+        expect("aids%d" % k, npart, [row("IDSP", k, 256)])
+        expect("ainf%d" % k, npart, [C(inf[k], 2048, 4096)])
+        expect("ast%d" % k, npart, [C("POOL", 2048, 4096)])
+        for h in (0, 1):
+            mm(V("PS%d" % h), V("IB"), row("TC", h, 512), True, False)
+        src, o16 = ("POOL", 0.0) if k == 0 else ("V16", 24576.0)
+        for j in range(16):
+            mm(C("PS2", 0, 128), V("IB"), C(src, j, 2048, 16), j == 0, j == 15)
+        C16 = C("E1O", 0, 128)
+        ts(C16, C("PS2", 0, 128), -o16, None, ADD)
+        for h in (0, 1):
+            b = "PS%d" % h
+            mm(V(b), C16, row("BE", h, 512), False, False)
+            for i in range(4):
+                mm(row(b, i), row("NBE", 4 * h + i), C16, False, i == 3)
+        ts(V("CW"), C("PS2", 0, 128), 1.0 / 16, -o16 / 16, MUL, ADD)
+        for h in (0, 1):
+            ts(row("G", h, 512), V("PS%d" % h), 0.0, None, GT)
+        for gg in range(8):
+            mm(C("PS2", 128, 256), row("GS", gg), row("G", gg), gg == 0, gg == 7)
+        ts(C("E1O", 128, 256), C("PS2", 128, 256), 1.0 / 2048, None, MUL)
+        E1P = [row("E1P", 2 * k), row("E1P", 2 * k + 1)]
+        send(p, "ae1%d" % k, "le1", row("E1P", k, 256), V("E1O"))
+        send(p, "ast%d" % k, "lst", C("POOL", 2048, 4096), C("POOL", 0, 2048))
+        send(p, "ainf%d" % k, "linf", C(inf[k], 2048, 4096), C(inf[k], 0, 2048))
+        expect("ae1%d" % k, npart, [row("E1P", k, 256)])
+        for h in (0, 1):
+            mm(V("PS%d" % h), V("ONE"), row("G", h, 512), True, False)
+        if k > 0:
+            for a in range(0, 2048, 512):
+                b = "PS4" if a % 1024 == 0 else "PS7"
+                vsum(a, b)
+                vround(a, b)
+        else:
+            ts(V("TS"), V("GS"), V("PC"), None, MUL)
+        ttg(V("Y1"), V("CW"), V("CL"), C("POOL", 0, 2048), MAX)
+        if k == 0:
+            ts(V("QB"), V("QC"), -BIG, None, ADD)
+            ts(V("QB2"), V("QC2"), BIG, None, ADD)
+            ts(V("CD"), V("PC"), -16.0, 2048.0, MUL, ADD)
+            ts(V("CE"), V("PC"), 16.0, -2048.0, MUL, ADD)
+        KEY = C("PS3", 0, 128)
+        mm(KEY, V("IB"), V("QC" if isA else "QC2"), True, False)
+        mm(KEY, C16, V("BXN" if isA else "BXP"), False, False)
+        for j in range(16):
+            mm(C("PS3", j, 128, 16), C("Y1", j, 2048, 16), V("BP" if isA else "BN"), False, False)
+        for h in (0, 1):
+            mm(V("PS%d" % h), E1P[1], row("NBE", h, 512), False, True)
+        mm(C("PS6", 0, 128), E1P[0], V("BXP" if isA else "BXN"), True, True)
+        for h in (0, 1):
+            ts(row("MA", h, 512), V("PS%d" % h), 0.0, None, EQU)
+        ts(V("CPW"), E1P[0], 1.0 / 16, None, MUL)
+        for gg in range(8):
+            mm(C("PS2", 256, 384), row("TS", gg), row("MA", gg), gg == 0, gg == 7)
+        scopy(V("TPX"), C("PS6", 0, 128))
+        scopy(V("MAF"), V("MA"))
+        if k > 0:
+            for a in (2048, 3072):
+                vgath(a, a + 1024, prev)
+        vcopy(V("MLL"), C("PS2", 256, 384))
+        ttg(V("Y2"), V("CPW"), V("MLL"), C("POOL", 0, 2048), MAX)
+        for gg in range(8):
+            for w, u, x, n in ((gg, 0, 0, 16), (gg, 16, 0, 8), (gg + 8, 0, 8, 8), (gg + 8, 8, 0, 16)):
+                for c in (0, 1):
+                    i = 256 * k + 128 * c + 16 * gg + x
+                    mm(V("PS5", w, slice(u, u + n)), row("MA", gg), C("IDSP", i, i + n), c == 0, c == 1)
+        for gg in range(8):
+            mm(row("PS3", gg, 16), row("MAF", gg), row("TPX", gg, 16), False, False)
+        for j in range(16):
+            mm(C("PS3", j, 128, 16), C("Y2", j, 2048, 16), V("BN" if isA else "BP"), False, j == 15)
+        for r in range(8):
+            tt(row("EQ", r, 256), V("PS5", ALL, slice(r, r + 16)), V("IDO"), EQU)
+        for r in range(16):
+            mm(C("PS4", 0, 128), V("IB"), row("EQ", r), r == 0, r == 15)
+        if k > 0:
+            for a in range(2048, 4096, 512):
+                b = "PS%d" % (a // 512 % 2)
+                vsum(a, b)
+                vround(a, b)
+        ts(V("NC"), C("PS4", 0, 128), -1.0, 1.0, MUL, ADD)
+        tt(V("CB"), C("PS4", 0, 128), V("QB" if isA else "QB2"), MUL)
+        tt(V("K1"), KEY, V("NC"), MUL)
+        tt(V("SRA"), V("K1"), V("CB"), ADD)
+        desc = not isA
+        stage("SRA", "SRB", 1, 2, desc)
+        stage("SRB", "SRA", 2, 4, desc)
+        stage("SRA", "SRB", 1, 4, desc)
+        stage("SRB", "SRA", 4, 8, desc)
+        stage("SRA", "SRB", 2, 8, desc)
+        stage("SRB", "SRA", 1, 8, desc)
+        merge("SRA", "SRB", "E2O", desc)
+        send(p, "ae2%d" % k, "le2", row("E2P", k), V("E2O"))
+        expect("ae2%d" % k, npart, [row("E2P", k)])
+        for gg in range(8):
+            mm(row("PS6", 8 + gg, 16), row("MA", gg), V("TC16"), True, True)
+        TP = C("PS6", 128, 256)
+        if isA:
+            ts(V("DIF"), TP, 16.0, V("CD"), MUL, ADD)
+            adj = V("T16")
+        else:
+            ts(V("DIF"), TP, -16.0, V("CE"), MUL, ADD)
+            ts(V("ADJ"), TP, 16.0, 2048.0, MUL, ADD)
+            adj = V("ADJ")
+        mm(C("PS2", 384, 512), adj, V("IF"), True, False)
+        for gg in range(8):
+            mm(row("PS7", 8 + gg, 16), row("MAF", gg), row("E2P", 8 * k + gg, 16), True, True)
+        tt(V("SRA"), V("E2O"), C("PS7", 128, 256), MIN if isA else MAX)
+        if isA:
+            merge("SRA", "SRB", "SRA")
+            ts(V("SRB"), V("SRA"), -3000000.0, 2 * BIG, LT, MUL)
+            tt(V("SRM"), V("SRA"), V("SRB"), ADD)
+            merge("SRM", "SRB", "SI")
+        else:
+            merge("SRA", "SRB", "SI")
+        ts(V("BB"), V("SI"), 4, 1, SHR, AND)
+        ts(V("QA"), V("SI"), 15, None, AND)
+        tt(V("M1"), V("BB"), V("DIF"), MUL)
+        tt(V("A1"), V("M1"), V("QA"), ADD)
+        mm(C("PS2", 384, 512), V("A1"), V("IF"), False, True)
+        vcopy(V("LST"), C("PS2", 384, 512))
+        tab = "ALLT0" if k == 1 else "ALLT1"
+        m0 = 2048 * me
+        vgather(C(tab, m0, m0 + 1024), V("POOL"), C("LST", 0, 64))
+        sgather(C(tab, m0 + 1024, m0 + 2048), V("POOL"), C("LST", 64, 128))
+        prev = tab
+        if k < 2:
+            send_all("ae3%d" % k, "le3", blk(tab, me))
+            expect("ae3%d" % k, NB * (nrank - 1), [blk(tab, r) for r in others])
+            vcopy(C("V16", 0, 1024), C(tab, m0, m0 + 1024))
+            sgather(C(inf[k + 1], 0, 2048), V(inf[k]), V("LST"))
+            info_done(k + 1, DS[k + 1])
+            ttg(V("SU"), V(tab), C("PAL", 0, 64), C("V16", 0, 1024), ADD)
+            sgather(C("REP", 4096, 5120), V(tab), C("PAL", 64, 128))
+            for a in (0, 1024):
+                vgath(a, a + 1024, tab)
+            for h in (0, 1):
+                mm(V("PS%d" % h), V("IB"), C(tab, m0 + 1024 + 512 * h, m0 + 1536 + 512 * h), True, False)
+                mm(V("PS%d" % h), V("IB"), row("REP", 8 + h, 512), False, True)
+            ts(C("V16", 0, 1024), V("SU"), 0.5, 1536.25, MUL, ADD)
+            for h in (0, 1):
+                ts(row("V16", 2 + h, 512), V("PS%d" % h), 0.5, 1536.25, MUL, ADD)
+            ts(C("POOL", 0, 2048), V("V16"), -1536.0, None, ADD)
+        else:
+            def put(i):
+                dma("y", "dyx%d" % i, None, row("YXO", i, 1024), ext_out=T.yx[:, 1024 * i:1024 * i + 1024])
+            for a in (2048, 3072):
+                vgath(a, a + 1024, tab)
+            for a in range(2048, 4096, 512):
+                vsum(a, "PS%d" % (a // 512 % 4))
+            for a in range(2048, 4096, 512):
+                vround(a, "PS%d" % (a // 512 % 4), C("YXO", a, a + 512), 128.0)
+            vdve(0, 1024, tab)
+            put(0)
+            put(2)
+            vdve(1024, 2048, tab)
+            put(1)
+            put(3)
+            vgather(C(inf[k + 1], 0, 2048), V(inf[k]), V("LST"))
+            info_done(k + 1, None)
+            mm(C("PS7", 0, 128), V("IDO", slice(0, 8)), V("IF"), True, True)
+            scopy(V("YLO"), C("PS7", 0, 128))
+            dma("y", "dyl", None, V("YLO"), ext_out=T.yl[:, :])
+    for sem in sorted(tot):
+        if know["g"].get(sem, 0) < tot[sem]:
+            g.wait_ge(T.sem[sem], tot[sem])

@@ -17,7 +17,7 @@ _SB = {
     "E1O": ([128, 256], FH), "E1P": ([128, 768], FH), "CW": ([128, 128], FF), "CPW": ([128, 128], FF),
     "G": ([128, 1024], BF), "MA": ([128, 1024], BF), "MAF": ([128, 1024], FF), "MLL": ([128, 128], U2), "TPX": ([128, 128], FF),
     "IDSO": ([128, 256], BF), "IDSP": ([128, 768], BF), "IDO": ([128, 16, 16], FF), "PAF": ([128, 128], FF), "PAL": ([128, 128], U2),
-    "Y1": ([128, 2048], FH), "Y2": ([128, 2048], FH), "EQ": ([128, 2048], BF),
+    "Y1": ([128, 2048], FH), "Y2": ([128, 2048], FH), "EQ": ([128, 2048], BF), "IDX": ([128, 32, 32], BF),
     "NC": ([128, 128], FF), "CB": ([128, 128], FF), "K1": ([128, 128], FF),
     "SRA": (S6, FF), "SRB": (S6, FF), "SRM": (S6, FF), "E2O": ([128, 128], FF), "E2P": ([128, 384], FF),
     "SI": ([128, 128], I4), "QA": ([128, 128], I4), "BB": ([128, 128], I4), "M1": ([128, 128], FF), "A1": ([128, 128], FF),
@@ -34,7 +34,7 @@ SCRATCH = {k: ("sbuf", s, d) for k, (s, d) in _SB.items()}
 _PS = {"PS%d" % i: ([128, 16, 32] if i == 5 else [128, 512], FF) for i in range(8)}
 for _k, (_s, _d) in _PS.items():
     SCRATCH[_k] = ("psum", _s, _d)
-SEMAPHORES = (["cv", "cs", "ct", "cg", "dsl", "dpr", "dx0", "dx1", "dpw0", "dpw1", "dyl"] + ["dyx%d" % i for i in range(4)]
+SEMAPHORES = (["cv", "cs", "ct", "cg", "dsl", "dpr", "dx0", "dx1", "dpw0", "dpw1", "dyl"] + ["dyx%d" % i for i in range(6)]
               + ["ali%d" % i for i in range(4)] + ["arep%d" % i for i in range(4)]
               + ["apt", "lli", "lpt", "lrep", "linf", "lids", "lst", "le1", "le2", "le3"]
               + [n + str(k) for n in ("ainf", "aids", "ast", "ae1", "ae2", "ae3") for k in range(3)])
@@ -204,11 +204,11 @@ def rank_program(g, core, T, topo):
     def mm(out, l, r, start, stop):
         op("t", lambda: g.tensor.matmul(out["ap"], l["ap"], r["ap"], start, stop), [l, r], [out])
 
-    def iota(out, pattern, cm, small=True):
+    def iota(out, pattern, cm, small=True, base=0):
         if small:
-            op("g", lambda: g.iota(out["ap"], pattern, 0, cm, allow_small_or_imprecise_dtypes=True), [], [out])
+            op("g", lambda: g.iota(out["ap"], pattern, base, cm, allow_small_or_imprecise_dtypes=True), [], [out])
         else:
-            op("g", lambda: g.iota(out["ap"], pattern, 0, cm), [], [out])
+            op("g", lambda: g.iota(out["ap"], pattern, base, cm), [], [out])
 
     def afs(out, a, pattern, cmp, base, cm):
         op("g", lambda: g.affine_select(out["ap"], a["ap"], pattern, cmp, 0.0, base, cm), [a], [out])
@@ -226,6 +226,8 @@ def rank_program(g, core, T, topo):
     fill(V("ONE"), 1.0)
     fill(C("XW", 0, 16), 0.0)
     fill(C("XW", 4112, 4128), 0.0)
+    fill(C("PWIN", 0, 4096), 0.0)
+    scopy(C("PWIN", 4096, 8192), C("PWIN", 0, 4096))
     iota(V("PC"), [[0, 1]], 1)
     iota(V("PCI"), [[0, 1]], 1, False)
     afs(V("B8a"), C("ONE", 0, 8), [[-16, 8]], GE, 0, 1)
@@ -238,7 +240,6 @@ def rank_program(g, core, T, topo):
     def offsets(q):
         ts(row("OFF", q), row("LISTS", q), 16.0 - 4096.0 * me, 4112.0, ADD, MIN)
     offsets(me)
-    vcopy(V("PREYL"), V("PR"))
     ts(V("w0"), V("PR"), 2048 * me, None, ADD)
     ts(V("w1"), V("w0"), 7, None, SHR)
     ts(V("w2"), V("w0"), 127, None, AND)
@@ -249,19 +250,15 @@ def rank_program(g, core, T, topo):
     iota(V("QC"), [[0, 8], [1, 16]], 0)
     iota(V("TC16"), [[0, 16]], 1)
     iota(V("T16"), [[0, 128]], 16)
-    fill(C("PWIN", 0, 4096), 0.0)
     for r in others:
         expect("ali%d" % r, NB, [row("LISTS", r)])
     expect("apt", NB * (nrank - 1), [row("PT", r, 512) for r in others])
-    scopy(C("PWIN", 4096, 8192), C("PWIN", 0, 4096))
-    ts(V("P16I"), V("PCI"), 15, None, AND)
-    vcopy(V("P16"), V("P16I"))
-    ts(V("w3"), V("N16"), V("P16"), None, ADD)
-    ts(V("w4"), V("w3"), 127, None, AND)
-    vcopy(C("IDT", 1024, 1280), V("w4"))
-    ts(V("w4"), V("w3"), 7, None, SHR)
-    for o in range(nrank):
-        ts(row("IDT", o, 256), V("w4"), 32 * o, None, ADD)
+    for i in range(8):
+        ts(row("BE", i), V("ONE"), C("B8", i, i + 1), 128.0, MUL, MUL)
+    ts(V("NBE"), V("BE"), -1.0, None, MUL)
+    fill(V("GS"), 0.0)
+    for i in range(8):
+        fill(C("GS", 144 * i, 144 * i + 16), 1.0)
     order = [off[me % 2], off[1 - me % 2], on[0]]
     for q in order:
         offsets(q)
@@ -271,10 +268,25 @@ def rank_program(g, core, T, topo):
         send(order[i], "arep%d" % me, "lrep", blk("ALLT0", me), row("REP", i, 2048))
     for r in others:
         expect("arep%d" % r, ecount(r), [blk("ALLT0", r)])
-    vgather(blk("ALLT0", me), V("XW"), row("OFF", me))
+    vgather(row("ALLT0", 2 * me, 1024), V("XW"), row("OFF", 2 * me, 64))
+    sgather(row("ALLT0", 2 * me + 1, 1024), V("XW"), row("OFF", 2 * me + 1, 64))
     iota(V("TC"), [[0, 8], [1, 128]], -1)
+    iota(V("QC2"), [[0, 8], [1, 16]], 0, base=16)
+    iota(V("QB"), [[0, 8], [1, 16]], 0, base=-int(BIG))
+    iota(V("QB2"), [[0, 8], [1, 16]], 0, base=int(BIG) + 16)
+    iota(V("CD"), [[0, 1]], -16, base=2048)
+    iota(V("CE"), [[0, 1]], 16, base=-2048)
     fill(C("PWIN", 8192, 12288), 0.0)
-    fill(C("PWIN", 12288, 16384), 0.0)
+    scopy(C("PWIN", 12288, 16384), C("PWIN", 0, 4096))
+    ts(V("P16I"), V("PCI"), 15, None, AND)
+    vcopy(V("P16"), V("P16I"))
+    ts(V("w3"), V("N16"), V("P16"), None, ADD)
+    ts(V("w4"), V("w3"), 127, None, AND)
+    vcopy(C("IDT", 1024, 1280), V("w4"))
+    ts(V("w4"), V("w3"), 7, None, SHR)
+    vcopy(row("IDT", 0, 256), V("w4"))
+    for o in range(1, nrank):
+        scopy(row("IDT", o, 256), row("IDT", 0, 256), bias=32.0 * o)
 
     for c in range(4):
         for o in range(nrank):
@@ -295,22 +307,16 @@ def rank_program(g, core, T, topo):
     tt(C("WC", 5, 6), C("WC", 2, 3), C("WC", 3, 4), ADD)
     for c, w in enumerate((0, 1, 4, 5)):
         ts(row("SEL", c, 8), V("B8"), C("WC", w, w + 1), None, MUL)
-    for i in range(8):
-        ts(row("BE", i), V("ONE"), C("B8", i, i + 1), 128.0, MUL, MUL)
-    ts(V("NBE"), V("BE"), -1.0, None, MUL)
-    fill(V("GS"), 0.0)
-    for i in range(8):
-        fill(C("GS", 144 * i, 144 * i + 16), 1.0)
     vcopy(V("CL"), V("CLI"))
     fill(V("HALF"), 0.5)
+    vcopy(V("IF"), V("IB"))
     for i in range(8):
         ts(row("BXP", i, 16), C("ONE", 0, 16), C("B8", i, i + 1), 32.0, MUL, MUL)
     ts(V("BXN"), V("BXP"), -1.0, None, MUL)
     ts(V("BP"), V("B8"), 1024.0, None, MUL)
     ts(V("BN"), V("B8"), -1024.0, None, MUL)
-    vcopy(V("IF"), V("IB"))
-    ts(V("QC2"), V("QC"), 16.0, None, ADD)
-
+    ts(V("TS"), V("GS"), V("PC"), None, MUL)
+    vcopy(V("PREYL"), V("PR"))
     inf = ["INF0", "INF1", "INF2", "INF3"]
 
     def info_done(k, nxt):
@@ -327,11 +333,8 @@ def rank_program(g, core, T, topo):
         if nxt is not None:
             scopy(V("IDO", slice(8, 16)), C("PS4", 256, 384))
 
-    sgather(C("INF0", 0, 2048), V("PWIN"), V("ILST"))
     banks = ("PS0", "PS1", "PS6", "PS7")
     for n, r in enumerate([me] + on + off):
-        if n == 3:
-            info_done(0, DS[0])
         for i, b in enumerate(banks):
             mm(V(b), V("IB"), row("ALLT0", 4 * r + i, 512), n == 0, n == 3)
     for i, b in enumerate(banks):
@@ -339,7 +342,7 @@ def rank_program(g, core, T, topo):
             ts(row("POOL", i, 512), V(b), -128.0, None, ADD)
         else:
             scopy(row("POOL", i, 512), V(b), bias=-128.0)
-    scopy(V("V"), C("XW", 16, 4112), bias=-128.0)
+    sgather(C("INF0", 0, 2048), V("PWIN"), V("ILST"))
 
     def vgath(a, b, tab):
         sgather(C("REP", a, b), blk(tab, me), C("PREYL", a // 16, b // 16))
@@ -397,8 +400,9 @@ def rank_program(g, core, T, topo):
         for h in (0, 1):
             mm(V("PS%d" % h), V("IB"), row("TC", h, 512), True, False)
         src, o16 = ("POOL", 0.0) if k == 0 else ("V16", 24576.0)
-        for j in range(16):
-            mm(C("PS2", 0, 128), V("IB"), C(src, j, 2048, 16), j == 0, j == 15)
+        for h in (0, 1):
+            for j in range(16):
+                mm(row("PS2", h, 64), V("IB"), C(src, 1024 * h + j, 1024 * h + 1024, 16), j == 0, j == 15)
         C16 = C("E1O", 0, 128)
         ts(C16, C("PS2", 0, 128), -o16, None, ADD)
         for h in (0, 1):
@@ -414,24 +418,22 @@ def rank_program(g, core, T, topo):
         ts(C("E1O", 128, 256), C("PS2", 128, 256), 1.0 / 2048, None, MUL)
         E1P = [row("E1P", 2 * k), row("E1P", 2 * k + 1)]
         send(p, "ae1%d" % k, "le1", row("E1P", k, 256), V("E1O"))
+        for h in (0, 1):
+            mm(V("PS%d" % h), V("ONE"), row("G", h, 512), True, False)
+        if k == 0:
+            info_done(0, d)
         send(p, "ast%d" % k, "lst", C("POOL", 2048, 4096), C("POOL", 0, 2048))
         send(p, "ainf%d" % k, "linf", C(inf[k], 2048, 4096), C(inf[k], 0, 2048))
         expect("ae1%d" % k, npart, [row("E1P", k, 256)])
-        for h in (0, 1):
-            mm(V("PS%d" % h), V("ONE"), row("G", h, 512), True, False)
+        scopy(V("IDX", slice(0, 16), slice(0, 16)), row("IDSP", k, 256))
+        scopy(V("IDX", slice(16, 32), slice(8, 24)), row("IDSP", k, 256))
+        scopy(V("IDX", slice(0, 16), slice(16, 24)), V("IDX", slice(0, 16), slice(0, 8)))
+        scopy(V("IDX", slice(16, 32), slice(0, 8)), V("IDX", slice(0, 16), slice(8, 16)))
         if k > 0:
-            for a in range(0, 2048, 512):
-                b = "PS4" if a % 1024 == 0 else "PS7"
+            for a, b in ((0, "PS4"), (512, "PS7")):
                 vsum(a, b)
                 vround(a, b)
-        else:
-            ts(V("TS"), V("GS"), V("PC"), None, MUL)
         ttg(V("Y1"), V("CW"), V("CL"), C("POOL", 0, 2048), MAX)
-        if k == 0:
-            ts(V("QB"), V("QC"), -BIG, None, ADD)
-            ts(V("QB2"), V("QC2"), BIG, None, ADD)
-            ts(V("CD"), V("PC"), -16.0, 2048.0, MUL, ADD)
-            ts(V("CE"), V("PC"), 16.0, -2048.0, MUL, ADD)
         KEY = C("PS3", 0, 128)
         mm(KEY, V("IB"), V("QC" if isA else "QC2"), True, False)
         mm(KEY, C16, V("BXN" if isA else "BXP"), False, False)
@@ -447,16 +449,17 @@ def rank_program(g, core, T, topo):
             mm(C("PS2", 256, 384), row("TS", gg), row("MA", gg), gg == 0, gg == 7)
         scopy(V("TPX"), C("PS6", 0, 128))
         scopy(V("MAF"), V("MA"))
-        if k > 0:
-            for a in (2048, 3072):
-                vgath(a, a + 1024, prev)
+        if k == 0:
+            scopy(V("V"), C("XW", 16, 4112), bias=-128.0)
         vcopy(V("MLL"), C("PS2", 256, 384))
         ttg(V("Y2"), V("CPW"), V("MLL"), C("POOL", 0, 2048), MAX)
         for gg in range(8):
-            for w, u, x, n in ((gg, 0, 0, 16), (gg, 16, 0, 8), (gg + 8, 0, 8, 8), (gg + 8, 8, 0, 16)):
+            for u in (0, 1):
                 for c in (0, 1):
-                    i = 256 * k + 128 * c + 16 * gg + x
-                    mm(V("PS5", w, slice(u, u + n)), row("MA", gg), C("IDSP", i, i + n), c == 0, c == 1)
+                    mm(V("PS5", 8 * u + gg, slice(0, 24)), row("MA", gg), V("IDX", 16 * u + 8 * c + gg, slice(0, 24)), c == 0, c == 1)
+        if k > 0:
+            for a in (2048, 3072):
+                vgath(a, a + 1024, prev)
         for gg in range(8):
             mm(row("PS3", gg, 16), row("MAF", gg), row("TPX", gg, 16), False, False)
         for j in range(16):
@@ -466,7 +469,7 @@ def rank_program(g, core, T, topo):
         for r in range(16):
             mm(C("PS4", 0, 128), V("IB"), row("EQ", r), r == 0, r == 15)
         if k > 0:
-            for a in range(2048, 4096, 512):
+            for a in range(1024, 4096, 512):
                 b = "PS%d" % (a // 512 % 2)
                 vsum(a, b)
                 vround(a, b)
@@ -534,25 +537,34 @@ def rank_program(g, core, T, topo):
                 ts(row("V16", 2 + h, 512), V("PS%d" % h), 0.5, 1536.25, MUL, ADD)
             ts(C("POOL", 0, 2048), V("V16"), -1536.0, None, ADD)
         else:
-            def put(i):
-                dma("y", "dyx%d" % i, None, row("YXO", i, 1024), ext_out=T.yx[:, 1024 * i:1024 * i + 1024])
+            def put(i, a, b):
+                dma("y", "dyx%d" % i, None, C("YXO", a, b), ext_out=T.yx[:, a:b])
+
+            def last(a):
+                vround(a, "PS%d" % (a // 512 % 4), C("YXO", a, a + 512), 128.0)
             for a in (2048, 3072):
                 vgath(a, a + 1024, tab)
+            sgather(C("INF3", 1536, 2048), V(inf[k]), C("LST", 96, 128))
             for a in range(2048, 4096, 512):
                 vsum(a, "PS%d" % (a // 512 % 4))
-            for a in range(2048, 4096, 512):
-                vround(a, "PS%d" % (a // 512 % 4), C("YXO", a, a + 512), 128.0)
             vdve(0, 1024, tab)
-            put(0)
-            put(2)
-            vdve(1024, 2048, tab)
-            put(1)
-            put(3)
-            vgather(C(inf[k + 1], 0, 2048), V(inf[k]), V("LST"))
-            info_done(k + 1, None)
+            put(0, 0, 1024)
+            vgather(C("INF3", 0, 1536), V(inf[k]), C("LST", 0, 96))
+            last(2048)
+            last(2560)
+            put(1, 2048, 3072)
+            vdve(1024, 1536, tab)
+            put(2, 1024, 1536)
+            info_done(3, None)
             mm(C("PS7", 0, 128), V("IDO", slice(0, 8)), V("IF"), True, True)
             scopy(V("YLO"), C("PS7", 0, 128))
             dma("y", "dyl", None, V("YLO"), ext_out=T.yl[:, :])
+            vdve(1536, 2048, tab)
+            put(3, 1536, 2048)
+            last(3072)
+            put(4, 3072, 3584)
+            last(3584)
+            put(5, 3584, 4096)
     for sem in sorted(tot):
         if know["g"].get(sem, 0) < tot[sem]:
             g.wait_ge(T.sem[sem], tot[sem])

@@ -12,13 +12,15 @@ _SB = {
     "PT": ([128, 2048], BF), "IDT": ([128, 1280], BF), "PWIN": ([128, 16384], BF),
     "ALLT0": ([128, 8192], BF), "ALLT1": ([128, 8192], BF), "POOL": ([128, 4096], BF),
     "INF0": ([128, 4096], BF), "INF1": ([128, 4096], BF), "INF2": ([128, 4096], BF), "INF3": ([128, 2048], BF),
-    "V": ([128, 4096], BF), "VS": ([128, 2048], FH), "VT": ([128, 2048], FH), "VM": ([128, 1024], FF), "HALF": ([128, 512], BF),
+    "V": ([128, 4096], FH), "VS": ([128, 2048], FH), "VT": ([128, 2048], FH),
+    "NH": ([128, 128], BF), "IBP": ([128, 128], BF), "IBN": ([128, 128], BF), "AMX": ([128, 128], FF),
     "YXO": ([128, 4096], FF), "SU": ([128, 1024], FH), "V16": ([128, 2048], FH),
     "E1O": ([128, 256], FH), "E1P": ([128, 768], FH), "CW": ([128, 128], FF), "CPW": ([128, 128], FF),
-    "G": ([128, 1024], BF), "MA": ([128, 1024], BF), "MAF": ([128, 1024], FF), "MLL": ([128, 128], U2), "TPX": ([128, 128], FF),
+    "G": ([128, 1024], BF), "MA": ([128, 1024], BF), "MAF": ([128, 1024], FF), "MLL": ([128, 128], U2),
+    "TPH": ([128, 128], FH), "TPL": ([128, 128], FH), "B8N": ([128, 8], BF), "BYP": ([128, 128], BF), "BYN": ([128, 128], BF),
     "IDSO": ([128, 256], BF), "IDSP": ([128, 768], BF), "IDO": ([128, 16, 16], FF), "PAF": ([128, 128], FF), "PAL": ([128, 128], U2),
     "Y1": ([128, 2048], FH), "Y2": ([128, 2048], FH), "EQ": ([128, 2048], BF), "IDX": ([128, 32, 32], BF),
-    "NC": ([128, 128], FF), "CB": ([128, 128], FF), "K1": ([128, 128], FF),
+    "K1": ([128, 128], FF),
     "SRA": (S6, FF), "SRB": (S6, FF), "SRM": (S6, FF), "E2O": ([128, 128], FF), "E2P": ([128, 384], FF),
     "SI": ([128, 128], I4), "QA": ([128, 128], I4), "BB": ([128, 128], I4), "M1": ([128, 128], FF), "A1": ([128, 128], FF),
     "DIF": ([128, 128], FF), "ADJ": ([128, 128], FF), "LST": ([128, 128], U2), "YLO": ([128, 128], FF),
@@ -26,7 +28,7 @@ _SB = {
     "B8a": ([128, 8], BF), "B8": ([128, 8], BF), "BE": ([128, 1024], BF), "NBE": ([128, 1024], BF),
     "GS": ([128, 1024], BF), "TS": ([128, 1024], BF), "PC": ([128, 1], FF), "PCI": ([128, 1], I4), "P16I": ([128, 1], I4),
     "P16": ([128, 1], FF), "CD": ([128, 1], FF), "CE": ([128, 1], FF), "T16": ([128, 128], FF), "TC16": ([128, 16], BF),
-    "QC": ([128, 128], BF), "QC2": ([128, 128], BF), "QB": ([128, 128], FF), "QB2": ([128, 128], FF),
+    "QC": ([128, 128], BF), "QC2": ([128, 128], BF),
     "BP": ([128, 8], FH), "BN": ([128, 8], FH), "BXP": ([128, 128], BF), "BXN": ([128, 128], BF),
     "WC": ([128, 8], FF), "SEL": ([128, 32], BF), "CLI": ([128, 128], I4), "CL": ([128, 128], U2), "N16": ([128, 256], I4),
 }
@@ -39,13 +41,13 @@ SEMAPHORES = (["cv", "cs", "ct", "cg", "dsl", "dpr", "dx0", "dx1", "dpw0", "dpw1
               + ["apt", "lli", "lpt", "lrep", "linf", "lids", "lst", "le1", "le2", "le3"]
               + [n + str(k) for n in ("ainf", "aids", "ast", "ae1", "ae2", "ae3") for k in range(3)])
 
-ADD, MUL, MAX, MIN = AluOpType.add, AluOpType.mult, AluOpType.max, AluOpType.min
+ADD, SUB, MUL = AluOpType.add, AluOpType.subtract, AluOpType.mult
+MAX, MIN = AluOpType.max, AluOpType.min
 GT, GE, LT, EQU = AluOpType.is_gt, AluOpType.is_ge, AluOpType.is_lt, AluOpType.is_equal
 SHR, AND = AluOpType.arith_shift_right, AluOpType.bitwise_and
 COPY = ActivationFunctionType.Copy
 ALL = slice(None)
 BIG = 4194304.0
-MAGIC = 12582912.0
 DS = (1, 2, 3)
 
 
@@ -156,11 +158,12 @@ def rank_program(g, core, T, topo):
     def ecount(src):
         return len(topo.engines(cores[src], core))
 
-    def send(r, sem, lsem, dst, src):
+    def send(r, sem, lsem, dst, src, es=None):
         need("g", touch("g", [src], []))
         rid, pid, _ = topo.addr(cores[r])
-        ev = done("g", lsem, len(topo.engines(core, cores[r])))
-        g.remote_dma(dst["ap"], src["ap"], T.sem[sem], T.sem[lsem], pid, rid, topo.mask(core, cores[r]))
+        es = es or topo.engines(core, cores[r])
+        ev = done("g", lsem, len(es))
+        g.remote_dma(dst["ap"], src["ap"], T.sem[sem], T.sem[lsem], pid, rid, sum(1 << e for e in es))
         note("g", [src], [], ev)
 
     def send_all(sem, lsem, x):
@@ -226,8 +229,9 @@ def rank_program(g, core, T, topo):
     fill(V("ONE"), 1.0)
     fill(C("XW", 0, 16), 0.0)
     fill(C("XW", 4112, 4128), 0.0)
-    fill(C("PWIN", 0, 4096), 0.0)
-    scopy(C("PWIN", 4096, 8192), C("PWIN", 0, 4096))
+    fill(C("PWIN", 0, 2048), 0.0)
+    scopy(C("PWIN", 2048, 4096), C("PWIN", 0, 2048))
+    scopy(C("PWIN", 4096, 6144), C("PWIN", 0, 2048))
     iota(V("PC"), [[0, 1]], 1)
     iota(V("PCI"), [[0, 1]], 1, False)
     afs(V("B8a"), C("ONE", 0, 8), [[-16, 8]], GE, 0, 1)
@@ -253,31 +257,6 @@ def rank_program(g, core, T, topo):
     for r in others:
         expect("ali%d" % r, NB, [row("LISTS", r)])
     expect("apt", NB * (nrank - 1), [row("PT", r, 512) for r in others])
-    for i in range(8):
-        ts(row("BE", i), V("ONE"), C("B8", i, i + 1), 128.0, MUL, MUL)
-    ts(V("NBE"), V("BE"), -1.0, None, MUL)
-    fill(V("GS"), 0.0)
-    for i in range(8):
-        fill(C("GS", 144 * i, 144 * i + 16), 1.0)
-    order = [off[me % 2], off[1 - me % 2], on[0]]
-    for q in order:
-        offsets(q)
-    for i, q in enumerate(order):
-        (sgather if i != 1 else vgather)(row("REP", i, 2048), V("XW"), row("OFF", q))
-    for i in range(3):
-        send(order[i], "arep%d" % me, "lrep", blk("ALLT0", me), row("REP", i, 2048))
-    for r in others:
-        expect("arep%d" % r, ecount(r), [blk("ALLT0", r)])
-    vgather(row("ALLT0", 2 * me, 1024), V("XW"), row("OFF", 2 * me, 64))
-    sgather(row("ALLT0", 2 * me + 1, 1024), V("XW"), row("OFF", 2 * me + 1, 64))
-    iota(V("TC"), [[0, 8], [1, 128]], -1)
-    iota(V("QC2"), [[0, 8], [1, 16]], 0, base=16)
-    iota(V("QB"), [[0, 8], [1, 16]], 0, base=-int(BIG))
-    iota(V("QB2"), [[0, 8], [1, 16]], 0, base=int(BIG) + 16)
-    iota(V("CD"), [[0, 1]], -16, base=2048)
-    iota(V("CE"), [[0, 1]], 16, base=-2048)
-    fill(C("PWIN", 8192, 12288), 0.0)
-    scopy(C("PWIN", 12288, 16384), C("PWIN", 0, 4096))
     ts(V("P16I"), V("PCI"), 15, None, AND)
     vcopy(V("P16"), V("P16I"))
     ts(V("w3"), V("N16"), V("P16"), None, ADD)
@@ -285,13 +264,36 @@ def rank_program(g, core, T, topo):
     vcopy(C("IDT", 1024, 1280), V("w4"))
     ts(V("w4"), V("w3"), 7, None, SHR)
     vcopy(row("IDT", 0, 256), V("w4"))
+    order = [off[me % 2], off[1 - me % 2], on[0]]
+    for i, q in enumerate(order):
+        offsets(q)
+        vgather(row("REP", 2 * i, 1024), V("XW"), row("OFF", 2 * q, 64))
+        sgather(row("REP", 2 * i + 1, 1024), V("XW"), row("OFF", 2 * q + 1, 64))
+        send(q, "arep%d" % me, "lrep", blk("ALLT0", me), row("REP", i, 2048), e_on if q in on else e_off)
+    for r in others:
+        expect("arep%d" % r, NB, [blk("ALLT0", r)])
+    vgather(row("ALLT0", 2 * me, 1024), V("XW"), row("OFF", 2 * me, 64))
+    sgather(row("ALLT0", 2 * me + 1, 1024), V("XW"), row("OFF", 2 * me + 1, 64))
+    iota(V("TC"), [[0, 8], [1, 128]], -1)
+    iota(V("QC2"), [[0, 8], [1, 16]], 0, base=16)
+    iota(V("CD"), [[0, 1]], -16, base=2048)
+    iota(V("CE"), [[0, 1]], 16, base=-2048)
+    fill(C("PWIN", 6144, 12288), 0.0)
     for o in range(1, nrank):
         scopy(row("IDT", o, 256), row("IDT", 0, 256), bias=32.0 * o)
+    scopy(C("PWIN", 12288, 16384), C("PWIN", 0, 4096))
 
-    for c in range(4):
-        for o in range(nrank):
+    for o in range(nrank):
+        for c in range(4):
             src = row("IDT", o if c == 0 else 4, 256) if c < 2 else row("PT", 2 * o + c - 2, 256)
             dma("y", "dpw%d" % (c // 2), C("PWIN", 4096 * o, 4096 * o + 4096, ps=slice(c, 128, 16), tag=c), src)
+    for i in range(8):
+        ts(row("BE", i), V("ONE"), C("B8", i, i + 1), 128.0, MUL, MUL)
+    ts(V("NBE"), V("BE"), -1.0, None, MUL)
+    ts(V("B8N"), V("B8"), -128.0, None, MUL)
+    fill(V("GS"), 0.0)
+    for i in range(8):
+        fill(C("GS", 144 * i, 144 * i + 16), 1.0)
     ts(V("q0"), V("SL"), 4, None, SHR)
     ts(V("q1"), V("SL"), 15, None, AND)
     ts(V("q2"), V("SL"), 12, None, SHR)
@@ -300,23 +302,30 @@ def rank_program(g, core, T, topo):
     tt(V("q0"), V("q0"), V("q1"), ADD)
     tt(V("q0"), V("q0"), V("q2"), ADD)
     vcopy(V("ILST"), V("q0"))
-
-    for c, (e, w) in enumerate(((0.0, 128.0), (1.0, 1.0), (2.0, 128.0), (3.0, 1.0))):
-        ts(C("WC", c, c + 1), V("P16"), e, w, EQU, MUL)
-    tt(C("WC", 4, 5), C("WC", 0, 1), C("WC", 1, 2), ADD)
-    tt(C("WC", 5, 6), C("WC", 2, 3), C("WC", 3, 4), ADD)
-    for c, w in enumerate((0, 1, 4, 5)):
-        ts(row("SEL", c, 8), V("B8"), C("WC", w, w + 1), None, MUL)
-    vcopy(V("CL"), V("CLI"))
-    fill(V("HALF"), 0.5)
-    vcopy(V("IF"), V("IB"))
     for i in range(8):
         ts(row("BXP", i, 16), C("ONE", 0, 16), C("B8", i, i + 1), 32.0, MUL, MUL)
     ts(V("BXN"), V("BXP"), -1.0, None, MUL)
+    ts(V("BYP"), V("BXP"), 1.0 / 32, None, MUL)
+    ts(V("BYN"), V("BXP"), -1.0 / 32, None, MUL)
     ts(V("BP"), V("B8"), 1024.0, None, MUL)
     ts(V("BN"), V("B8"), -1024.0, None, MUL)
-    ts(V("TS"), V("GS"), V("PC"), None, MUL)
-    vcopy(V("PREYL"), V("PR"))
+    vcopy(V("CL"), V("CLI"))
+
+    banks = ("PS3", "PS4", "PS6", "PS7")
+    mychip = sorted(on + [me])
+    for n, r in enumerate([me] + on + sorted(off, key=lambda r: mychip[r % 2] != me)):
+        for i, b in enumerate(banks):
+            mm(V(b), V("IB"), row("ALLT0", 4 * r + i, 512), n == 0, n == 3)
+    for i, b in enumerate(banks):
+        if i % 2 == 0:
+            ts(row("POOL", i, 512), V(b), -128.0, None, ADD)
+        else:
+            scopy(row("POOL", i, 512), V(b), bias=-128.0)
+
+    def ranks_open():
+        for h in (0, 1):
+            mm(V("PS%d" % h), V("IB"), row("TC", h, 512), True, False)
+
     inf = ["INF0", "INF1", "INF2", "INF3"]
 
     def info_done(k, nxt):
@@ -333,33 +342,19 @@ def rank_program(g, core, T, topo):
         if nxt is not None:
             scopy(V("IDO", slice(8, 16)), C("PS4", 256, 384))
 
-    banks = ("PS0", "PS1", "PS6", "PS7")
-    for n, r in enumerate([me] + on + off):
-        for i, b in enumerate(banks):
-            mm(V(b), V("IB"), row("ALLT0", 4 * r + i, 512), n == 0, n == 3)
-    for i, b in enumerate(banks):
-        if i % 2 == 0:
-            ts(row("POOL", i, 512), V(b), -128.0, None, ADD)
-        else:
-            scopy(row("POOL", i, 512), V(b), bias=-128.0)
-    sgather(C("INF0", 0, 2048), V("PWIN"), V("ILST"))
-
     def vgath(a, b, tab):
         sgather(C("REP", a, b), blk(tab, me), C("PREYL", a // 16, b // 16))
 
     def vsum(a, bank):
-        mm(V(bank), V("IB"), V("HALF"), True, False)
-        mm(V(bank), V("IB"), C("V", a, a + 512), False, False)
+        mm(V(bank), V("IB"), C("V", a, a + 512), True, False)
         mm(V(bank), V("IB"), C("REP", a, a + 512), False, True)
 
-    def vround(a, bank, out=None, add=0.0):
-        m = C("VM", a % 1024, a % 1024 + 512)
-        scopy(m, V(bank), scale=0.5, bias=MAGIC)
-        scopy(C("V", a, a + 512) if out is None else out, m, bias=add - MAGIC)
+    def vround(a, bank):
+        scopy(C("V", a, a + 512), V(bank), scale=0.5, bias=768.25)
 
     def vdve(a, b, tab):
         ttg(C("VS", a, b), blk(tab, me), C("PREYL", a // 16, b // 16), C("V", a, b), ADD)
-        ts(C("VT", a, b), C("VS", a, b), 0.5, 1536.25, MUL, ADD)
+        ts(C("VT", a, b), C("VS", a, b), 0.5, 768.25, MUL, ADD)
         ts(C("YXO", a, b), C("VT", a, b), -1408.0, None, ADD)
 
     bits = {1: 5, 2: 4, 4: 3, 8: 2}
@@ -389,7 +384,6 @@ def rank_program(g, core, T, topo):
         stage(src, other, 2, None, desc)
         stage(other, last, 1, None, desc)
 
-    prev = None
     for k, d in enumerate(DS):
         p = me ^ d
         isA = me < p
@@ -397,86 +391,102 @@ def rank_program(g, core, T, topo):
         expect("aids%d" % k, npart, [row("IDSP", k, 256)])
         expect("ainf%d" % k, npart, [C(inf[k], 2048, 4096)])
         expect("ast%d" % k, npart, [C("POOL", 2048, 4096)])
-        for h in (0, 1):
-            mm(V("PS%d" % h), V("IB"), row("TC", h, 512), True, False)
         src, o16 = ("POOL", 0.0) if k == 0 else ("V16", 24576.0)
         for h in (0, 1):
             for j in range(16):
                 mm(row("PS2", h, 64), V("IB"), C(src, 1024 * h + j, 1024 * h + 1024, 16), j == 0, j == 15)
+        if k == 0:
+            ranks_open()
+            sgather(C("INF0", 0, 2048), V("PWIN"), V("ILST"))
         C16 = C("E1O", 0, 128)
         ts(C16, C("PS2", 0, 128), -o16, None, ADD)
-        for h in (0, 1):
-            b = "PS%d" % h
-            mm(V(b), C16, row("BE", h, 512), False, False)
-            for i in range(4):
-                mm(row(b, i), row("NBE", 4 * h + i), C16, False, i == 3)
+        mm(C("PS6", 384, 392), C16, V("B8N"), True, True)
+        for gg in range(8):
+            mm(row("PS%d" % (gg // 4), gg % 4), row("NBE", gg), C16, False, gg % 4 == 3)
         ts(V("CW"), C("PS2", 0, 128), 1.0 / 16, -o16 / 16, MUL, ADD)
-        for h in (0, 1):
-            ts(row("G", h, 512), V("PS%d" % h), 0.0, None, GT)
+        if k == 0:
+            for c, (e, w) in enumerate(((0.0, 128.0), (1.0, 1.0), (2.0, 128.0), (3.0, 1.0))):
+                ts(C("WC", c, c + 1), V("P16"), e, w, EQU, MUL)
+            tt(C("WC", 4, 5), C("WC", 0, 1), C("WC", 1, 2), ADD)
+            tt(C("WC", 5, 6), C("WC", 2, 3), C("WC", 3, 4), ADD)
+            for c, w in enumerate((0, 1, 4, 5)):
+                ts(row("SEL", c, 8), V("B8"), C("WC", w, w + 1), None, MUL)
+        for gg in range(8):
+            ts(row("G", gg), row("PS%d" % (gg // 4), gg % 4), C("PS6", 384 + gg, 385 + gg), None, GT)
         for gg in range(8):
             mm(C("PS2", 128, 256), row("GS", gg), row("G", gg), gg == 0, gg == 7)
         ts(C("E1O", 128, 256), C("PS2", 128, 256), 1.0 / 2048, None, MUL)
         E1P = [row("E1P", 2 * k), row("E1P", 2 * k + 1)]
         send(p, "ae1%d" % k, "le1", row("E1P", k, 256), V("E1O"))
+        if k == 0:
+            ts(V("TS"), V("GS"), V("PC"), 1.0 / 32, MUL, MUL)
+            ts(V("IBP"), V("IB"), 2 * BIG, None, MUL)
+            ts(V("IBN"), V("IB"), -2 * BIG, None, MUL)
+            fill(V("NH"), -0.5)
         for h in (0, 1):
             mm(V("PS%d" % h), V("ONE"), row("G", h, 512), True, False)
         if k == 0:
             info_done(0, d)
+        else:
+            vsum(0, "PS4")
+            vsum(512, "PS7")
         send(p, "ast%d" % k, "lst", C("POOL", 2048, 4096), C("POOL", 0, 2048))
         send(p, "ainf%d" % k, "linf", C(inf[k], 2048, 4096), C(inf[k], 0, 2048))
         expect("ae1%d" % k, npart, [row("E1P", k, 256)])
-        scopy(V("IDX", slice(0, 16), slice(0, 16)), row("IDSP", k, 256))
-        scopy(V("IDX", slice(16, 32), slice(8, 24)), row("IDSP", k, 256))
+        scopy(V("IDX", slice(0, 16), slice(0, 16)), row("IDSP", k, 256), scale=1.0 / 32)
+        scopy(V("IDX", slice(16, 32), slice(8, 24)), row("IDSP", k, 256), scale=1.0 / 32)
         scopy(V("IDX", slice(0, 16), slice(16, 24)), V("IDX", slice(0, 16), slice(0, 8)))
         scopy(V("IDX", slice(16, 32), slice(0, 8)), V("IDX", slice(0, 16), slice(8, 16)))
-        if k > 0:
-            for a, b in ((0, "PS4"), (512, "PS7")):
-                vsum(a, b)
-                vround(a, b)
-        ttg(V("Y1"), V("CW"), V("CL"), C("POOL", 0, 2048), MAX)
+        ttg(C("Y1", 0, 1024), V("CW"), C("CL", 0, 64), C("POOL", 0, 1024), MAX)
+        ttg(C("Y1", 1024, 2048), V("CW"), C("CL", 64, 128), C("POOL", 1024, 2048), MAX)
         KEY = C("PS3", 0, 128)
         mm(KEY, V("IB"), V("QC" if isA else "QC2"), True, False)
         mm(KEY, C16, V("BXN" if isA else "BXP"), False, False)
+        for h in (0, 1):
+            mm(V("PS%d" % h), E1P[1], row("NBE", h, 512), False, True)
+        mm(C("PS6", 0, 128), E1P[0], V("BYP" if isA else "BYN"), True, True)
         for j in range(16):
             mm(C("PS3", j, 128, 16), C("Y1", j, 2048, 16), V("BP" if isA else "BN"), False, False)
         for h in (0, 1):
-            mm(V("PS%d" % h), E1P[1], row("NBE", h, 512), False, True)
-        mm(C("PS6", 0, 128), E1P[0], V("BXP" if isA else "BXN"), True, True)
-        for h in (0, 1):
-            ts(row("MA", h, 512), V("PS%d" % h), 0.0, None, EQU)
+            ts(row("MA", h, 512), V("PS%d" % h), 0.0, 32.0, EQU, MUL)
         ts(V("CPW"), E1P[0], 1.0 / 16, None, MUL)
         for gg in range(8):
             mm(C("PS2", 256, 384), row("TS", gg), row("MA", gg), gg == 0, gg == 7)
-        scopy(V("TPX"), C("PS6", 0, 128))
-        scopy(V("MAF"), V("MA"))
-        if k == 0:
-            scopy(V("V"), C("XW", 16, 4112), bias=-128.0)
+        scopy(V("TPH"), C("PS6", 0, 128))
+        tt(V("TPL"), C("PS6", 0, 128), V("TPH"), SUB)
+        scopy(V("MAF"), V("MA"), scale=1.0 / 32)
+        if k > 0:
+            vround(0, "PS4")
+            vround(512, "PS7")
         vcopy(V("MLL"), C("PS2", 256, 384))
         ttg(V("Y2"), V("CPW"), V("MLL"), C("POOL", 0, 2048), MAX)
         for gg in range(8):
-            for u in (0, 1):
-                for c in (0, 1):
-                    mm(V("PS5", 8 * u + gg, slice(0, 24)), row("MA", gg), V("IDX", 16 * u + 8 * c + gg, slice(0, 24)), c == 0, c == 1)
-        if k > 0:
-            for a in (2048, 3072):
-                vgath(a, a + 1024, prev)
+            for c in (0, 1):
+                mm(V("PS5", slice(gg, 16, 8), slice(0, 24)), row("MA", gg), V("IDX", slice(8 * c + gg, 32, 16), slice(0, 24)),
+                   c == 0, c == 1)
         for gg in range(8):
-            mm(row("PS3", gg, 16), row("MAF", gg), row("TPX", gg, 16), False, False)
+            for piece in ("TPH", "TPL"):
+                mm(row("PS3", gg, 16), row("MA", gg), row(piece, gg, 16), False, False)
         for j in range(16):
             mm(C("PS3", j, 128, 16), C("Y2", j, 2048, 16), V("BN" if isA else "BP"), False, j == 15)
+        IW, KC = (V("IBN"), "QC") if isA else (V("IBP"), "QC2")
+        CM = C("PS4", 0, 128)
+        mm(CM, V("IB"), V(KC), True, False)
+        mm(CM, IW, V("NH"), False, False)
         for r in range(8):
             tt(row("EQ", r, 256), V("PS5", ALL, slice(r, r + 16)), V("IDO"), EQU)
-        for r in range(16):
-            mm(C("PS4", 0, 128), V("IB"), row("EQ", r), r == 0, r == 15)
-        if k > 0:
-            for a in range(1024, 4096, 512):
-                b = "PS%d" % (a // 512 % 2)
-                vsum(a, b)
-                vround(a, b)
-        ts(V("NC"), C("PS4", 0, 128), -1.0, 1.0, MUL, ADD)
-        tt(V("CB"), C("PS4", 0, 128), V("QB" if isA else "QB2"), MUL)
-        tt(V("K1"), KEY, V("NC"), MUL)
-        tt(V("SRA"), V("K1"), V("CB"), ADD)
+            for h in (0, 1):
+                mm(CM, IW, row("EQ", 2 * r + h), False, r == 7 and h == 1)
+            if r == 6:
+                vcopy(V("K1"), KEY)
+        tt(V("SRA"), V("K1"), CM, MIN if isA else MAX)
+        if k == 0:
+            scopy(V("V"), C("XW", 16, 4112), bias=1408.0)
+            vcopy(V("IF"), V("IB"))
+        else:
+            for i, b in ((2, "PS0"), (3, "PS1"), (4, "PS3")):
+                vsum(512 * i, b)
+                vround(512 * i, b)
         desc = not isA
         stage("SRA", "SRB", 1, 2, desc)
         stage("SRB", "SRA", 2, 4, desc)
@@ -487,26 +497,37 @@ def rank_program(g, core, T, topo):
         merge("SRA", "SRB", "E2O", desc)
         send(p, "ae2%d" % k, "le2", row("E2P", k), V("E2O"))
         expect("ae2%d" % k, npart, [row("E2P", k)])
+        if k == 0:
+            vcopy(V("PREYL"), V("PR"))
         for gg in range(8):
             mm(row("PS6", 8 + gg, 16), row("MA", gg), V("TC16"), True, True)
         TP = C("PS6", 128, 256)
         if isA:
-            ts(V("DIF"), TP, 16.0, V("CD"), MUL, ADD)
+            ts(V("DIF"), TP, 0.5, V("CD"), MUL, ADD)
             adj = V("T16")
         else:
-            ts(V("DIF"), TP, -16.0, V("CE"), MUL, ADD)
-            ts(V("ADJ"), TP, 16.0, 2048.0, MUL, ADD)
+            ts(V("DIF"), TP, -0.5, V("CE"), MUL, ADD)
+            ts(V("ADJ"), TP, 0.5, 2048.0, MUL, ADD)
             adj = V("ADJ")
         mm(C("PS2", 384, 512), adj, V("IF"), True, False)
+        if isA:
+            ts(V("SRB"), V("E2O"), -3000000.0, 2 * BIG, LT, MUL)
+            tt(V("SRM"), V("E2O"), V("SRB"), ADD)
+            merge("SRM", "SRB", "SRM")
+            ts(V("SRB"), V("SRM"), 3000000.0, -2 * BIG, LT, MUL)
+            tt(V("AMX"), V("SRM"), V("SRB"), ADD)
         for gg in range(8):
             mm(row("PS7", 8 + gg, 16), row("MAF", gg), row("E2P", 8 * k + gg, 16), True, True)
-        tt(V("SRA"), V("E2O"), C("PS7", 128, 256), MIN if isA else MAX)
+        if k > 0:
+            for i, b in ((5, "PS0"), (6, "PS1"), (7, "PS4"))[:2 if k < 2 else 3]:
+                vsum(512 * i, b)
+                vround(512 * i, b)
         if isA:
+            tt(V("SRA"), V("SRM"), C("PS7", 128, 256), MIN)
             merge("SRA", "SRB", "SRA")
-            ts(V("SRB"), V("SRA"), -3000000.0, 2 * BIG, LT, MUL)
-            tt(V("SRM"), V("SRA"), V("SRB"), ADD)
-            merge("SRM", "SRB", "SI")
+            tt(V("SI"), V("SRA"), V("AMX"), MAX)
         else:
+            tt(V("SRA"), V("E2O"), C("PS7", 128, 256), MAX)
             merge("SRA", "SRB", "SI")
         ts(V("BB"), V("SI"), 4, 1, SHR, AND)
         ts(V("QA"), V("SI"), 15, None, AND)
@@ -518,30 +539,36 @@ def rank_program(g, core, T, topo):
         m0 = 2048 * me
         vgather(C(tab, m0, m0 + 1024), V("POOL"), C("LST", 0, 64))
         sgather(C(tab, m0 + 1024, m0 + 2048), V("POOL"), C("LST", 64, 128))
-        prev = tab
         if k < 2:
             send_all("ae3%d" % k, "le3", blk(tab, me))
             expect("ae3%d" % k, NB * (nrank - 1), [blk(tab, r) for r in others])
             vcopy(C("V16", 0, 1024), C(tab, m0, m0 + 1024))
             sgather(C(inf[k + 1], 0, 2048), V(inf[k]), V("LST"))
+            if k > 0:
+                vsum(3584, "PS0")
             info_done(k + 1, DS[k + 1])
+            if k > 0:
+                vround(3584, "PS0")
+            ranks_open()
             ttg(V("SU"), V(tab), C("PAL", 0, 64), C("V16", 0, 1024), ADD)
             sgather(C("REP", 4096, 5120), V(tab), C("PAL", 64, 128))
-            for a in (0, 1024):
-                vgath(a, a + 1024, tab)
             for h in (0, 1):
-                mm(V("PS%d" % h), V("IB"), C(tab, m0 + 1024 + 512 * h, m0 + 1536 + 512 * h), True, False)
-                mm(V("PS%d" % h), V("IB"), row("REP", 8 + h, 512), False, True)
+                mm(V("PS%d" % (6 + h)), V("IB"), C(tab, m0 + 1024 + 512 * h, m0 + 1536 + 512 * h), True, False)
+            for h in (0, 1):
+                mm(V("PS%d" % (6 + h)), V("IB"), row("REP", 8 + h, 512), False, True)
             ts(C("V16", 0, 1024), V("SU"), 0.5, 1536.25, MUL, ADD)
-            for h in (0, 1):
-                ts(row("V16", 2 + h, 512), V("PS%d" % h), 0.5, 1536.25, MUL, ADD)
+            ts(row("V16", 2, 512), V("PS6"), 0.5, 1536.25, MUL, ADD)
+            scopy(row("V16", 3, 512), V("PS7"), scale=0.5, bias=1536.25)
+            for a in (0, 1024, 2048, 3072):
+                vgath(a, a + 1024, tab)
             ts(C("POOL", 0, 2048), V("V16"), -1536.0, None, ADD)
         else:
             def put(i, a, b):
                 dma("y", "dyx%d" % i, None, C("YXO", a, b), ext_out=T.yx[:, a:b])
 
             def last(a):
-                vround(a, "PS%d" % (a // 512 % 4), C("YXO", a, a + 512), 128.0)
+                vround(a, "PS%d" % (a // 512 % 4))
+                scopy(C("YXO", a, a + 512), C("V", a, a + 512), bias=-1408.0)
             for a in (2048, 3072):
                 vgath(a, a + 1024, tab)
             sgather(C("INF3", 1536, 2048), V(inf[k]), C("LST", 96, 128))

@@ -15,22 +15,24 @@ _SB = {
     "V": ([128, 4096], FH), "VS": ([128, 2048], FH), "VT": ([128, 2048], FH),
     "NH": ([128, 128], BF), "IBP": ([128, 128], BF), "IBN": ([128, 128], BF), "AMX": ([128, 128], FF),
     "YXO": ([128, 4096], FF), "SU": ([128, 1024], FH), "V16": ([128, 2048], FH),
-    "E1O": ([128, 256], FH), "E1P": ([128, 768], FH), "CW": ([128, 128], FF), "CPW": ([128, 128], FF),
-    "G": ([128, 1024], BF), "MA": ([128, 1024], BF), "MAF": ([128, 1024], FF), "MLL": ([128, 128], U2),
-    "TPH": ([128, 128], FH), "TPL": ([128, 128], FH), "B8N": ([128, 8], BF), "BYP": ([128, 128], BF), "BYN": ([128, 128], BF),
+    "E1O": ([128, 256], FH), "E1P": ([128, 768], FH), "C16": ([128, 128], FH), "E16": ([128, 2048], BF),
+    "CSM": ([128, 128], FH), "CBT": ([128, 128], FH),
+    "G": ([128, 1024], BF), "MA": ([128, 1024], BF), "MAF": ([128, 1024], FF),
+    "B8N": ([128, 8], BF), "B8P": ([128, 8], BF),
     "IDSO": ([128, 256], BF), "IDSP": ([128, 768], BF), "IDO": ([128, 16, 16], FF), "PAF": ([128, 128], FF), "PAL": ([128, 128], U2),
     "Y1": ([128, 2048], FH), "Y2": ([128, 2048], FH), "EQ": ([128, 2048], BF), "IDX": ([128, 32, 32], BF),
     "K1": ([128, 128], FF),
     "SRA": (S6, FF), "SRB": (S6, FF), "SRM": (S6, FF), "E2O": ([128, 128], FF), "E2P": ([128, 384], FF),
-    "SI": ([128, 128], I4), "QA": ([128, 128], I4), "BB": ([128, 128], I4), "M1": ([128, 128], FF), "A1": ([128, 128], FF),
-    "DIF": ([128, 128], FF), "ADJ": ([128, 128], FF), "LST": ([128, 128], U2), "YLO": ([128, 128], FF),
+    "SI": ([128, 128], I4), "QA": ([128, 128], I4), "BB": ([128, 128], I4), "M1": ([128, 128], BF), "QAB": ([128, 128], BF),
+    "ADJ": ([128, 128], BF), "LST": ([128, 128], U2), "YLO": ([128, 128], FF),
     "ONE": ([128, 128], BF), "IB": ([128, 128], BF), "IF": ([128, 128], FF), "TC": ([128, 1024], BF),
     "B8a": ([128, 8], BF), "B8": ([128, 8], BF), "BE": ([128, 1024], BF), "NBE": ([128, 1024], BF),
-    "GS": ([128, 1024], BF), "TS": ([128, 1024], BF), "PC": ([128, 1], FF), "PCI": ([128, 1], I4), "P16I": ([128, 1], I4),
-    "P16": ([128, 1], FF), "CD": ([128, 1], FF), "CE": ([128, 1], FF), "T16": ([128, 128], FF), "TC16": ([128, 16], BF),
+    "GS": ([128, 1024], BF), "PCI": ([128, 1], I4), "P16I": ([128, 1], I4),
+    "P16": ([128, 1], FF), "CE": ([128, 1], FF), "T16": ([128, 128], BF), "TC16": ([128, 16], BF), "TCN": ([128, 16], BF),
+    "TDI": ([128, 128], BF), "TD": ([128, 128], BF), "TDN": ([128, 128], BF),
     "QC": ([128, 128], BF), "QC2": ([128, 128], BF),
     "BP": ([128, 8], FH), "BN": ([128, 8], FH), "BXP": ([128, 128], BF), "BXN": ([128, 128], BF),
-    "WC": ([128, 8], FF), "SEL": ([128, 32], BF), "CLI": ([128, 128], I4), "CL": ([128, 128], U2), "N16": ([128, 256], I4),
+    "WC": ([128, 8], FF), "SEL": ([128, 32], BF), "N16": ([128, 256], I4),
 }
 SCRATCH = {k: ("sbuf", s, d) for k, (s, d) in _SB.items()}
 _PS = {"PS%d" % i: ([128, 16, 32] if i == 5 else [128, 512], FF) for i in range(8)}
@@ -39,6 +41,7 @@ for _k, (_s, _d) in _PS.items():
 SEMAPHORES = (["cv", "cs", "ct", "cg", "dsl", "dpr", "dx0", "dx1", "dpw0", "dpw1", "dyl"] + ["dyx%d" % i for i in range(6)]
               + ["ali%d" % i for i in range(4)] + ["arep%d" % i for i in range(4)]
               + ["apt", "lli", "lpt", "lrep", "linf", "lids", "lst", "le1", "le2", "le3"]
+              + ["ad3%d%d" % (k, h) for k in (0, 1) for h in (0, 1)]
               + [n + str(k) for n in ("ainf", "aids", "ast", "ae1", "ae2", "ae3") for k in range(3)])
 
 ADD, SUB, MUL = AluOpType.add, AluOpType.subtract, AluOpType.mult
@@ -150,6 +153,8 @@ def rank_program(g, core, T, topo):
     e_off = list(topo.engines(core, cores[off[0]]))
     e_on = [e for e in topo.engines(core, cores[on[0]]) if e not in e_off]
     NB = len(e_off)
+    far = off[me % 2]
+    e_hand = [e_on, list(topo.engines(core, cores[on[0]]))]
 
     def did(r):
         rid, pid, _ = topo.addr(cores[r])
@@ -166,13 +171,16 @@ def rank_program(g, core, T, topo):
         g.remote_dma(dst["ap"], src["ap"], T.sem[sem], T.sem[lsem], pid, rid, sum(1 << e for e in es))
         note("g", [src], [], ev)
 
-    def send_all(sem, lsem, x):
+    def send_parts(parts, lsem, x):
         need("g", touch("g", [x], []))
         tr = [RemoteDMATransfer(dst_ids=[did(r) for r in rs], dma_engine_mask=sum(1 << e for e in es), remote_sem=T.sem[sem],
-                                srcs=[x["ap"]], dsts=[x["ap"] for r in rs], alu_op=0) for rs, es in ((off, e_off), (on, e_on))]
-        ev = done("g", lsem, len(e_off) + len(e_on))
+                                srcs=[x["ap"]], dsts=[x["ap"] for r in rs], alu_op=0) for sem, rs, es in parts]
+        ev = done("g", lsem, sum(len(es) for _, _, es in parts))
         g.remote_dma_fused(tr, local_sem=T.sem[lsem])
         note("g", [x], [], ev)
+
+    def send_all(sem, lsem, x):
+        send_parts([(sem, off, e_off), (sem, on, e_on)], lsem, x)
 
     def ts(out, a, s1, s2, op0, op1=None):
         ins = [a] + [s for s in (s1, s2) if isinstance(s, dict)]
@@ -232,7 +240,6 @@ def rank_program(g, core, T, topo):
     fill(C("PWIN", 0, 2048), 0.0)
     scopy(C("PWIN", 2048, 4096), C("PWIN", 0, 2048))
     scopy(C("PWIN", 4096, 6144), C("PWIN", 0, 2048))
-    iota(V("PC"), [[0, 1]], 1)
     iota(V("PCI"), [[0, 1]], 1, False)
     afs(V("B8a"), C("ONE", 0, 8), [[-16, 8]], GE, 0, 1)
     afs(V("B8"), V("B8a"), [[16, 8]], GE, 15, -1)
@@ -250,7 +257,6 @@ def rank_program(g, core, T, topo):
     vcopy(C("PT", 512 * me, 512 * me + 256), V("w1"))
     vcopy(C("PT", 512 * me + 256, 512 * me + 512), V("w2"))
     send_all("apt", "lpt", row("PT", me, 512))
-    iota(V("CLI"), [[1, 128]], 0, False)
     iota(V("QC"), [[0, 8], [1, 16]], 0)
     iota(V("TC16"), [[0, 16]], 1)
     iota(V("T16"), [[0, 128]], 16)
@@ -264,7 +270,7 @@ def rank_program(g, core, T, topo):
     vcopy(C("IDT", 1024, 1280), V("w4"))
     ts(V("w4"), V("w3"), 7, None, SHR)
     vcopy(row("IDT", 0, 256), V("w4"))
-    order = [off[me % 2], off[1 - me % 2], on[0]]
+    order = [far, off[1 - me % 2], on[0]]
     for i, q in enumerate(order):
         offsets(q)
         vgather(row("REP", 2 * i, 1024), V("XW"), row("OFF", 2 * q, 64))
@@ -276,8 +282,10 @@ def rank_program(g, core, T, topo):
     sgather(row("ALLT0", 2 * me + 1, 1024), V("XW"), row("OFF", 2 * me + 1, 64))
     iota(V("TC"), [[0, 8], [1, 128]], -1)
     iota(V("QC2"), [[0, 8], [1, 16]], 0, base=16)
-    iota(V("CD"), [[0, 1]], -16, base=2048)
-    iota(V("CE"), [[0, 1]], 16, base=-2048)
+    iota(V("TDI"), [[-1, 128]], 0, base=128)
+    iota(V("CE"), [[0, 1]], 16)
+    fill(V("EQ"), 1.0 / 16)
+    afs(V("E16"), V("EQ"), [[-1, 128], [0, 16]], EQU, 0, 1)
     fill(C("PWIN", 6144, 12288), 0.0)
     for o in range(1, nrank):
         scopy(row("IDT", o, 256), row("IDT", 0, 256), bias=32.0 * o)
@@ -291,6 +299,7 @@ def rank_program(g, core, T, topo):
         ts(row("BE", i), V("ONE"), C("B8", i, i + 1), 128.0, MUL, MUL)
     ts(V("NBE"), V("BE"), -1.0, None, MUL)
     ts(V("B8N"), V("B8"), -128.0, None, MUL)
+    ts(V("B8P"), V("B8"), 128.0, None, MUL)
     fill(V("GS"), 0.0)
     for i in range(8):
         fill(C("GS", 144 * i, 144 * i + 16), 1.0)
@@ -305,11 +314,12 @@ def rank_program(g, core, T, topo):
     for i in range(8):
         ts(row("BXP", i, 16), C("ONE", 0, 16), C("B8", i, i + 1), 32.0, MUL, MUL)
     ts(V("BXN"), V("BXP"), -1.0, None, MUL)
-    ts(V("BYP"), V("BXP"), 1.0 / 32, None, MUL)
-    ts(V("BYN"), V("BXP"), -1.0 / 32, None, MUL)
     ts(V("BP"), V("B8"), 1024.0, None, MUL)
     ts(V("BN"), V("B8"), -1024.0, None, MUL)
-    vcopy(V("CL"), V("CLI"))
+    ts(V("TCN"), V("TC16"), -0.5, None, MUL)
+    ts(V("TC16"), V("TC16"), 0.5, None, MUL)
+    ts(V("TD"), V("TDI"), 0.125, None, MUL)
+    ts(V("TDN"), V("TDI"), -0.125, None, MUL)
 
     banks = ("PS3", "PS4", "PS6", "PS7")
     mychip = sorted(on + [me])
@@ -398,12 +408,12 @@ def rank_program(g, core, T, topo):
         if k == 0:
             ranks_open()
             sgather(C("INF0", 0, 2048), V("PWIN"), V("ILST"))
-        C16 = C("E1O", 0, 128)
+        C16 = V("C16")
         ts(C16, C("PS2", 0, 128), -o16, None, ADD)
         mm(C("PS6", 384, 392), C16, V("B8N"), True, True)
         for gg in range(8):
             mm(row("PS%d" % (gg // 4), gg % 4), row("NBE", gg), C16, False, gg % 4 == 3)
-        ts(V("CW"), C("PS2", 0, 128), 1.0 / 16, -o16 / 16, MUL, ADD)
+        mm(C("PS7", 0, 128), C16, V("IB"), True, True)
         if k == 0:
             for c, (e, w) in enumerate(((0.0, 128.0), (1.0, 1.0), (2.0, 128.0), (3.0, 1.0))):
                 ts(C("WC", c, c + 1), V("P16"), e, w, EQU, MUL)
@@ -413,23 +423,21 @@ def rank_program(g, core, T, topo):
                 ts(row("SEL", c, 8), V("B8"), C("WC", w, w + 1), None, MUL)
         for gg in range(8):
             ts(row("G", gg), row("PS%d" % (gg // 4), gg % 4), C("PS6", 384 + gg, 385 + gg), None, GT)
+        vcopy(C("E1O", 0, 128), C("PS7", 0, 128))
         for gg in range(8):
             mm(C("PS2", 128, 256), row("GS", gg), row("G", gg), gg == 0, gg == 7)
         ts(C("E1O", 128, 256), C("PS2", 128, 256), 1.0 / 2048, None, MUL)
-        E1P = [row("E1P", 2 * k), row("E1P", 2 * k + 1)]
         send(p, "ae1%d" % k, "le1", row("E1P", k, 256), V("E1O"))
         if k == 0:
-            ts(V("TS"), V("GS"), V("PC"), 1.0 / 32, MUL, MUL)
             ts(V("IBP"), V("IB"), 2 * BIG, None, MUL)
             ts(V("IBN"), V("IB"), -2 * BIG, None, MUL)
             fill(V("NH"), -0.5)
-        for h in (0, 1):
-            mm(V("PS%d" % h), V("ONE"), row("G", h, 512), True, False)
-        if k == 0:
             info_done(0, d)
-        else:
-            vsum(0, "PS4")
-            vsum(512, "PS7")
+        for i, b in enumerate(("PS5", "PS6", "PS7", "PS4")):
+            mm(V(b), C("E1O", 0, 128), row("E16", i, 512), True, True)
+            tt(row("Y1", i, 512), V(b), row("POOL", i, 512), MAX)
+        for h in (0, 1):
+            mm(V("PS%d" % h), V("ONE"), row("G", h, 512), True, True)
         send(p, "ast%d" % k, "lst", C("POOL", 2048, 4096), C("POOL", 0, 2048))
         send(p, "ainf%d" % k, "linf", C(inf[k], 2048, 4096), C(inf[k], 0, 2048))
         expect("ae1%d" % k, npart, [row("E1P", k, 256)])
@@ -437,44 +445,39 @@ def rank_program(g, core, T, topo):
         scopy(V("IDX", slice(16, 32), slice(8, 24)), row("IDSP", k, 256), scale=1.0 / 32)
         scopy(V("IDX", slice(0, 16), slice(16, 24)), V("IDX", slice(0, 16), slice(0, 8)))
         scopy(V("IDX", slice(16, 32), slice(0, 8)), V("IDX", slice(0, 16), slice(8, 16)))
-        ttg(C("Y1", 0, 1024), V("CW"), C("CL", 0, 64), C("POOL", 0, 1024), MAX)
-        ttg(C("Y1", 1024, 2048), V("CW"), C("CL", 64, 128), C("POOL", 1024, 2048), MAX)
         KEY = C("PS3", 0, 128)
         mm(KEY, V("IB"), V("QC" if isA else "QC2"), True, False)
         mm(KEY, C16, V("BXN" if isA else "BXP"), False, False)
-        for h in (0, 1):
-            mm(V("PS%d" % h), E1P[1], row("NBE", h, 512), False, True)
-        mm(C("PS6", 0, 128), E1P[0], V("BYP" if isA else "BYN"), True, True)
+        mm(C("PS6", 392, 400), row("E1P", 2 * k + 1), V("B8P"), True, True)
+        for gg in range(8):
+            ts(row("MA", gg), row("PS%d" % (gg // 4), gg % 4), C("PS6", 392 + gg, 393 + gg), 32.0, EQU, MUL)
         for j in range(16):
             mm(C("PS3", j, 128, 16), C("Y1", j, 2048, 16), V("BP" if isA else "BN"), False, False)
-        for h in (0, 1):
-            ts(row("MA", h, 512), V("PS%d" % h), 0.0, 32.0, EQU, MUL)
-        ts(V("CPW"), E1P[0], 1.0 / 16, None, MUL)
         for gg in range(8):
-            mm(C("PS2", 256, 384), row("TS", gg), row("MA", gg), gg == 0, gg == 7)
-        scopy(V("TPH"), C("PS6", 0, 128))
-        tt(V("TPL"), C("PS6", 0, 128), V("TPH"), SUB)
+            mm(C("PS2", 256 + 16 * gg, 272 + 16 * gg), row("MA", gg), row("E1P", 16 * k + gg, 16), True, True)
+        ts(V("CSM"), C("PS2", 256, 384), 1.0 / 32, None, MUL)
+        Y2B = ("PS0", "PS1", "PS4", "PS7")
+        for b in range(4):
+            mm(V(Y2B[b]), V("CSM"), row("E16", b, 512), True, True)
+        mm(C("PS6", 0, 128), V("CSM"), V("IB"), True, True)
+        scopy(V("CBT"), C("PS6", 0, 128))
         scopy(V("MAF"), V("MA"), scale=1.0 / 32)
-        if k > 0:
-            vround(0, "PS4")
-            vround(512, "PS7")
-        vcopy(V("MLL"), C("PS2", 256, 384))
-        ttg(V("Y2"), V("CPW"), V("MLL"), C("POOL", 0, 2048), MAX)
         for gg in range(8):
             for c in (0, 1):
                 mm(V("PS5", slice(gg, 16, 8), slice(0, 24)), row("MA", gg), V("IDX", slice(8 * c + gg, 32, 16), slice(0, 24)),
                    c == 0, c == 1)
-        for gg in range(8):
-            for piece in ("TPH", "TPL"):
-                mm(row("PS3", gg, 16), row("MA", gg), row(piece, gg, 16), False, False)
-        for j in range(16):
-            mm(C("PS3", j, 128, 16), C("Y2", j, 2048, 16), V("BN" if isA else "BP"), False, j == 15)
+        for b in range(4):
+            tt(row("Y2", b, 512), V(Y2B[b]), row("POOL", b, 512), MAX)
         IW, KC = (V("IBN"), "QC") if isA else (V("IBP"), "QC2")
-        CM = C("PS4", 0, 128)
+        CM = C("PS6", 384, 512)
+        mm(KEY, V("CBT"), V("BXP" if isA else "BXN"), False, False)
         mm(CM, V("IB"), V(KC), True, False)
         mm(CM, IW, V("NH"), False, False)
         for r in range(8):
             tt(row("EQ", r, 256), V("PS5", ALL, slice(r, r + 16)), V("IDO"), EQU)
+            if r == 0:
+                for j in range(16):
+                    mm(C("PS3", j, 128, 16), C("Y2", j, 2048, 16), V("BN" if isA else "BP"), False, j == 15)
             for h in (0, 1):
                 mm(CM, IW, row("EQ", 2 * r + h), False, r == 7 and h == 1)
             if r == 6:
@@ -484,7 +487,7 @@ def rank_program(g, core, T, topo):
             scopy(V("V"), C("XW", 16, 4112), bias=1408.0)
             vcopy(V("IF"), V("IB"))
         else:
-            for i, b in ((2, "PS0"), (3, "PS1"), (4, "PS3")):
+            for i, b in ((0, "PS4"), (1, "PS7"), (2, "PS0"), (3, "PS1"), (4, "PS3")):
                 vsum(512 * i, b)
                 vround(512 * i, b)
         desc = not isA
@@ -499,17 +502,15 @@ def rank_program(g, core, T, topo):
         expect("ae2%d" % k, npart, [row("E2P", k)])
         if k == 0:
             vcopy(V("PREYL"), V("PR"))
+        DIF = C("PS6", 128, 256)
+        mm(DIF, V("TD" if isA else "TDN"), V("ONE"), True, False)
         for gg in range(8):
-            mm(row("PS6", 8 + gg, 16), row("MA", gg), V("TC16"), True, True)
-        TP = C("PS6", 128, 256)
-        if isA:
-            ts(V("DIF"), TP, 0.5, V("CD"), MUL, ADD)
-            adj = V("T16")
-        else:
-            ts(V("DIF"), TP, -0.5, V("CE"), MUL, ADD)
-            ts(V("ADJ"), TP, 0.5, 2048.0, MUL, ADD)
+            mm(row("PS6", 8 + gg, 16), row("MA", gg), V("TC16" if isA else "TCN"), False, gg == 7)
+        adj = V("T16")
+        if not isA:
             adj = V("ADJ")
-        mm(C("PS2", 384, 512), adj, V("IF"), True, False)
+            ts(adj, DIF, -1.0, V("CE"), MUL, ADD)
+        mm(C("PS2", 384, 512), adj, V("IB"), True, False)
         if isA:
             ts(V("SRB"), V("E2O"), -3000000.0, 2 * BIG, LT, MUL)
             tt(V("SRM"), V("E2O"), V("SRB"), ADD)
@@ -518,8 +519,8 @@ def rank_program(g, core, T, topo):
             tt(V("AMX"), V("SRM"), V("SRB"), ADD)
         for gg in range(8):
             mm(row("PS7", 8 + gg, 16), row("MAF", gg), row("E2P", 8 * k + gg, 16), True, True)
-        if k > 0:
-            for i, b in ((5, "PS0"), (6, "PS1"), (7, "PS4"))[:2 if k < 2 else 3]:
+        if k == 2:
+            for i, b in ((5, "PS0"), (6, "PS1")):
                 vsum(512 * i, b)
                 vround(512 * i, b)
         if isA:
@@ -531,24 +532,37 @@ def rank_program(g, core, T, topo):
             merge("SRA", "SRB", "SI")
         ts(V("BB"), V("SI"), 4, 1, SHR, AND)
         ts(V("QA"), V("SI"), 15, None, AND)
-        tt(V("M1"), V("BB"), V("DIF"), MUL)
-        tt(V("A1"), V("M1"), V("QA"), ADD)
-        mm(C("PS2", 384, 512), V("A1"), V("IF"), False, True)
+        tt(V("M1"), V("BB"), DIF, MUL)
+        vcopy(V("QAB"), V("QA"))
+        mm(C("PS2", 384, 512), V("M1"), V("IB"), False, False)
+        mm(C("PS2", 384, 512), V("QAB"), V("IB"), False, True)
         vcopy(V("LST"), C("PS2", 384, 512))
         tab = "ALLT0" if k == 1 else "ALLT1"
         m0 = 2048 * me
-        vgather(C(tab, m0, m0 + 1024), V("POOL"), C("LST", 0, 64))
-        sgather(C(tab, m0 + 1024, m0 + 2048), V("POOL"), C("LST", 64, 128))
+        if k == 2:
+            vgather(C(tab, m0, m0 + 1024), V("POOL"), C("LST", 0, 64))
+            sgather(C(tab, m0 + 1024, m0 + 2048), V("POOL"), C("LST", 64, 128))
+        else:
+            for h in (0, 1):
+                a = m0 + 1024 * h
+                vgather(C(tab, a, a + 512), V("POOL"), C("LST", 64 * h, 64 * h + 32))
+                sgather(C(tab, a + 512, a + 1024), V("POOL"), C("LST", 64 * h + 32, 64 * h + 64))
+                send_parts([("ad3%d%d" % (k, h), [far], e_off), ("ae3%d" % k, on, e_on)], "le3", C(tab, a, a + 1024))
+            piece = [C(tab, 2048 * far + 1024 * h, 2048 * far + 1024 * h + 1024) for h in (0, 1)]
+            for h in (0, 1):
+                expect("ad3%d%d" % (k, h), NB, [piece[h]])
+            for h in (0, 1):
+                send(on[0], "ae3%d" % k, "le3", piece[h], piece[h], e_hand[h])
+            expect("ae3%d" % k, 2 * len(e_on) + len(e_hand[0]) + len(e_hand[1]), [blk(tab, r) for r in others if r != far])
         if k < 2:
-            send_all("ae3%d" % k, "le3", blk(tab, me))
-            expect("ae3%d" % k, NB * (nrank - 1), [blk(tab, r) for r in others])
             vcopy(C("V16", 0, 1024), C(tab, m0, m0 + 1024))
             sgather(C(inf[k + 1], 0, 2048), V(inf[k]), V("LST"))
-            if k > 0:
-                vsum(3584, "PS0")
+            late = ((5, "PS0"), (6, "PS1"), (7, "PS3")) if k > 0 else ()
+            for i, b in late:
+                vsum(512 * i, b)
             info_done(k + 1, DS[k + 1])
-            if k > 0:
-                vround(3584, "PS0")
+            for i, b in late:
+                vround(512 * i, b)
             ranks_open()
             ttg(V("SU"), V(tab), C("PAL", 0, 64), C("V16", 0, 1024), ADD)
             sgather(C("REP", 4096, 5120), V(tab), C("PAL", 64, 128))
@@ -569,8 +583,10 @@ def rank_program(g, core, T, topo):
             def last(a):
                 vround(a, "PS%d" % (a // 512 % 4))
                 scopy(C("YXO", a, a + 512), C("V", a, a + 512), bias=-1408.0)
-            for a in (2048, 3072):
-                vgath(a, a + 1024, tab)
+            vsum(3584, "PS4")
+            vgath(2048, 3072, tab)
+            vround(3584, "PS4")
+            vgath(3072, 4096, tab)
             sgather(C("INF3", 1536, 2048), V(inf[k]), C("LST", 96, 128))
             for a in range(2048, 4096, 512):
                 vsum(a, "PS%d" % (a // 512 % 4))

from concourse.bass import DstId, RemoteDMATransfer
from concourse.mybir import AluOpType, ActivationFunctionType

BF, FH, FF, I4, U2 = "bfloat16", "float16", "float32", "int32", "uint16"
S6 = [128, 8, 2, 2, 2, 2]
_SB = {
    "SL": ([128, 128], I4), "PR": ([128, 256], I4), "XW": ([128, 4128], BF),
    "LISTS": ([128, 512], U2), "OFF": ([128, 512], U2), "REP": ([128, 6144], BF),
    "PREYL": ([128, 256], U2), "ILST": ([128, 128], U2),
    "q0": ([128, 128], I4), "q1": ([128, 128], I4), "q2": ([128, 128], I4),
    "w0": ([128, 256], I4), "w1": ([128, 256], I4), "w2": ([128, 256], I4), "w3": ([128, 256], I4), "w4": ([128, 256], I4),
    "PT": ([128, 2048], BF), "IDT": ([128, 1280], BF), "PWIN": ([128, 16384], BF),
    "ALLT0": ([128, 8192], BF), "ALLT1": ([128, 8192], BF), "POOL": ([128, 4096], BF),
    "INF0": ([128, 4096], BF), "INF1": ([128, 4096], BF), "INF2": ([128, 4096], BF), "INF3": ([128, 2048], BF),
    "V": ([128, 4096], FH), "VS": ([128, 2048], FH), "VT": ([128, 2048], FH),
    "NH": ([128, 128], BF), "IBP": ([128, 128], BF), "IBN": ([128, 128], BF), "AMX": ([128, 128], FF),
    "YXO": ([128, 4096], FF), "SU": ([128, 1024], FH), "V16": ([128, 2048], FH),
    "E1O": ([128, 256], FH), "E1P": ([128, 768], FH), "C16": ([128, 128], FH), "E16": ([128, 2048], BF),
    "CSM": ([128, 128], FH), "CBT": ([128, 128], FH),
    "G": ([128, 1024], BF), "MA": ([128, 1024], BF), "MAF": ([128, 1024], FF),
    "B8N": ([128, 8], BF), "B8P": ([128, 8], BF),
    "IDSO": ([128, 256], BF), "IDSP": ([128, 768], BF), "IDO": ([128, 16, 16], FF), "PAF": ([128, 128], FF), "PAL": ([128, 128], U2),
    "Y1": ([128, 2048], FH), "Y2": ([128, 2048], FH), "EQ": ([128, 2048], BF), "IDX": ([128, 32, 32], BF),
    "K1": ([128, 128], FF),
    "SRA": (S6, FF), "SRB": (S6, FF), "SRM": (S6, FF), "E2O": ([128, 128], FF), "E2P": ([128, 384], FF),
    "SI": ([128, 128], I4), "QA": ([128, 128], I4), "BB": ([128, 128], I4), "M1": ([128, 128], BF), "QAB": ([128, 128], BF),
    "ADJ": ([128, 128], BF), "LST": ([128, 128], U2), "YLO": ([128, 128], FF),
    "ONE": ([128, 128], BF), "IB": ([128, 128], BF), "IF": ([128, 128], FF), "TC": ([128, 1024], BF),
    "B8a": ([128, 8], BF), "B8": ([128, 8], BF), "BE": ([128, 1024], BF), "NBE": ([128, 1024], BF),
    "GS": ([128, 1024], BF), "PCI": ([128, 1], I4), "P16I": ([128, 1], I4),
    "P16": ([128, 1], FF), "CE": ([128, 1], FF), "T16": ([128, 128], BF), "TC16": ([128, 16], BF), "TCN": ([128, 16], BF),
    "TDI": ([128, 128], BF), "TD": ([128, 128], BF), "TDN": ([128, 128], BF),
    "QC": ([128, 128], BF), "QC2": ([128, 128], BF),
    "BP": ([128, 8], FH), "BN": ([128, 8], FH), "BXP": ([128, 128], BF), "BXN": ([128, 128], BF),
    "WC": ([128, 8], FF), "SEL": ([128, 32], BF), "N16": ([128, 256], I4),
}
SCRATCH = {k: ("sbuf", s, d) for k, (s, d) in _SB.items()}
_PS = {"PS%d" % i: ([128, 16, 32] if i == 5 else [128, 512], FF) for i in range(8)}
for _k, (_s, _d) in _PS.items():
    SCRATCH[_k] = ("psum", _s, _d)
SEMAPHORES = (["cv", "cs", "ct", "cg", "dsl", "dpr", "dx0", "dx1", "dpw0", "dpw1", "dyl"] + ["dyx%d" % i for i in range(6)]
              + ["ali%d" % i for i in range(4)] + ["arep%d" % i for i in range(4)]
              + ["apt", "lli", "lpt", "lrep", "linf", "lids", "lst", "le1", "le2", "le3"]
              + ["ad3%d%d" % (k, h) for k in (0, 1) for h in (0, 1)]
              + [n + str(k) for n in ("ainf", "aids", "ast", "ae1", "ae2", "ae3") for k in range(3)])

ADD, SUB, MUL = AluOpType.add, AluOpType.subtract, AluOpType.mult
MAX, MIN = AluOpType.max, AluOpType.min
GT, GE, LT, EQU = AluOpType.is_gt, AluOpType.is_ge, AluOpType.is_lt, AluOpType.is_equal
SHR, AND = AluOpType.arith_shift_right, AluOpType.bitwise_and
COPY = ActivationFunctionType.Copy
ALL = slice(None)
BIG = 4194304.0
DS = (1, 2, 3)


def rank_program(g, core, T, topo):
    me = T.rank_of(core)
    if me is None:
        return
    cores = list(T.cores)
    nrank = len(cores)
    Q = {"v": g.vector, "s": g.scalar, "t": g.tensor, "g": g, "y": g.sync}
    know = {q: {} for q in Q}
    tot = {}
    log = {}

    def V(name, *idx, ps=ALL, tag=None):
        shape = SCRATCH[name][1][1:]
        st = [1] * len(shape)
        for i in range(len(shape) - 2, -1, -1):
            st[i] = st[i + 1] * shape[i + 1]
        full = list(idx) + [ALL] * (len(shape) - len(idx))
        m = 1
        for x, n, w in reversed(list(zip(full, shape, st))):
            r = range(x, x + 1) if isinstance(x, int) else range(*x.indices(n))
            if m == (1 << w) - 1 and r.step == 1:
                m = ((1 << (w * len(r))) - 1) << (w * r[0])
            else:
                m = sum(m << (i * w) for i in r)
        return {"ap": T[name][tuple([ps] + full)], "n": name, "m": m, "tag": tag}

    def C(name, a, b, step=1, **kw):
        return V(name, slice(a, b, step), **kw)

    def need(q, evs):
        for sem, cnt, sn in sorted(evs, key=lambda e: -len(e[2])):
            if know[q].get(sem, 0) >= cnt:
                continue
            c = tot[sem] if sem[0] in "dl" else cnt
            Q[q].wait_ge(T.sem[sem], c)
            k = know[q]
            for s_, c_ in list(sn.items()) + [(sem, c)]:
                if k.get(s_, 0) < c_:
                    k[s_] = c_

    def touch(q, ins, outs):
        evs = []
        for kind, lst in (("r", ins), ("w", outs)):
            for r in lst:
                if r["n"] in _PS:
                    d = log.setdefault(r["n"], {})
                    for oq in list(d):
                        if oq != q:
                            evs.append(d[oq])
                            del d[oq]
                    continue
                for e in log.get(r["n"], ()):
                    if not e[0] & r["m"] or (kind == "r" and e[2] == "r"):
                        continue
                    if e[1] is not None and r["tag"] is not None and e[1] != r["tag"]:
                        continue
                    evs.append(e[3])
        return evs

    def note(q, ins, outs, ev):
        for kind, lst in (("r", ins), ("w", outs)):
            for r in lst:
                if r["n"] in _PS:
                    log.setdefault(r["n"], {})[q] = ev
                    continue
                old = log.get(r["n"], [])
                if kind == "w":
                    old = [e for e in old if e[0] & ~r["m"] or (r["tag"] is not None and r["tag"] != e[1])]
                log[r["n"]] = old + [(r["m"], r["tag"], kind, ev)]

    def done(q, sem, n):
        tot[sem] = tot.get(sem, 0) + n
        d = dict(know[q])
        d[sem] = tot[sem]
        return (sem, tot[sem], d)

    def op(q, fn, ins, outs):
        need(q, touch(q, ins, outs))
        ev = done(q, "c" + q, 1)
        fn().then_inc(T.sem["c" + q], 1)
        note(q, ins, outs, ev)

    def dma(q, sem, out, in_, ext_out=None, ext_in=None):
        ins, outs = [in_] if in_ else [], [out] if out else []
        need(q, touch(q, ins, outs))
        ev = done(q, sem, 16)
        Q[q].dma_start(out["ap"] if out else ext_out, in_["ap"] if in_ else ext_in).then_inc(T.sem[sem], 16)
        note(q, ins, outs, ev)

    def expect(sem, cnt, outs):
        tot[sem] = tot.get(sem, 0) + cnt
        note("net", [], outs, (sem, tot[sem], {sem: tot[sem]}))

    others = [r for r in range(nrank) if r != me]
    off = [r for r in others if topo.chip(cores[r]) != topo.chip(core)]
    on = [r for r in others if r not in off]
    e_off = list(topo.engines(core, cores[off[0]]))
    e_on = [e for e in topo.engines(core, cores[on[0]]) if e not in e_off]
    NB = len(e_off)
    far = off[me % 2]
    e_hand = [e_on, list(topo.engines(core, cores[on[0]]))]

    def did(r):
        rid, pid, _ = topo.addr(cores[r])
        return DstId(rid=rid, pnc=pid)

    def ecount(src):
        return len(topo.engines(cores[src], core))

    def send(r, sem, lsem, dst, src, es=None):
        need("g", touch("g", [src], []))
        rid, pid, _ = topo.addr(cores[r])
        es = es or topo.engines(core, cores[r])
        ev = done("g", lsem, len(es))
        g.remote_dma(dst["ap"], src["ap"], T.sem[sem], T.sem[lsem], pid, rid, sum(1 << e for e in es))
        note("g", [src], [], ev)

    def send_parts(parts, lsem, x):
        need("g", touch("g", [x], []))
        tr = [RemoteDMATransfer(dst_ids=[did(r) for r in rs], dma_engine_mask=sum(1 << e for e in es), remote_sem=T.sem[sem],
                                srcs=[x["ap"]], dsts=[x["ap"] for r in rs], alu_op=0) for sem, rs, es in parts]
        ev = done("g", lsem, sum(len(es) for _, _, es in parts))
        g.remote_dma_fused(tr, local_sem=T.sem[lsem])
        note("g", [x], [], ev)

    def send_all(sem, lsem, x):
        send_parts([(sem, off, e_off), (sem, on, e_on)], lsem, x)

    def ts(out, a, s1, s2, op0, op1=None):
        ins = [a] + [s for s in (s1, s2) if isinstance(s, dict)]
        x1 = s1["ap"] if isinstance(s1, dict) else s1
        x2 = s2["ap"] if isinstance(s2, dict) else s2
        if op1 is None:
            op("v", lambda: g.vector.tensor_scalar(out["ap"], a["ap"], x1, None, op0), ins, [out])
        else:
            op("v", lambda: g.vector.tensor_scalar(out["ap"], a["ap"], x1, x2, op0, op1), ins, [out])

    def tt(out, a, b, o):
        op("v", lambda: g.vector.tensor_tensor(out["ap"], a["ap"], b["ap"], o), [a, b], [out])

    def ttg(out, win, lst, b, o):
        op("v", lambda: g.vector.tensor_tensor(out["ap"], win["ap"].indirect(lst["ap"]), b["ap"], o), [win, lst, b], [out])

    def vcopy(out, a):
        op("v", lambda: g.vector.tensor_copy(out["ap"], a["ap"]), [a], [out])

    def vgather(out, win, lst):
        op("v", lambda: g.vector.tensor_copy(out["ap"], win["ap"].indirect(lst["ap"])), [win, lst], [out])

    def sgather(out, win, lst):
        op("s", lambda: g.scalar.activation(out["ap"], win["ap"].indirect(lst["ap"]), COPY), [win, lst], [out])

    def scopy(out, a, bias=0.0, scale=1.0):
        op("s", lambda: g.scalar.activation(out["ap"], a["ap"], COPY, bias=bias, scale=scale), [a], [out])

    def fill(out, c):
        op("v", lambda: g.vector.memset(out["ap"], c), [], [out])

    def mm(out, l, r, start, stop):
        op("t", lambda: g.tensor.matmul(out["ap"], l["ap"], r["ap"], start, stop), [l, r], [out])

    def iota(out, pattern, cm, small=True, base=0):
        if small:
            op("g", lambda: g.iota(out["ap"], pattern, base, cm, allow_small_or_imprecise_dtypes=True), [], [out])
        else:
            op("g", lambda: g.iota(out["ap"], pattern, base, cm), [], [out])

    def afs(out, a, pattern, cmp, base, cm):
        op("g", lambda: g.affine_select(out["ap"], a["ap"], pattern, cmp, 0.0, base, cm), [a], [out])

    def blk(name, r):
        return C(name, 2048 * r, 2048 * r + 2048)

    def row(name, i, n=128):
        return C(name, n * i, n * i + n)

    dma("y", "dsl", V("SL"), None, ext_in=T.sl[:, :])
    dma("s", "dpr", V("PR"), None, ext_in=T.prey[:, :])
    dma("y", "dx0", C("XW", 16, 2064), None, ext_in=T.x[:, 0:2048])
    dma("s", "dx1", C("XW", 2064, 4112), None, ext_in=T.x[:, 2048:4096])
    fill(V("ONE"), 1.0)
    fill(C("XW", 0, 16), 0.0)
    fill(C("XW", 4112, 4128), 0.0)
    fill(C("PWIN", 0, 2048), 0.0)
    scopy(C("PWIN", 2048, 4096), C("PWIN", 0, 2048))
    scopy(C("PWIN", 4096, 6144), C("PWIN", 0, 2048))
    iota(V("PCI"), [[0, 1]], 1, False)
    afs(V("B8a"), C("ONE", 0, 8), [[-16, 8]], GE, 0, 1)
    afs(V("B8"), V("B8a"), [[16, 8]], GE, 15, -1)
    afs(V("IB"), V("ONE"), [[-1, 128]], EQU, 0, 1)
    iota(V("N16"), [[16, 256]], 0, False)
    vcopy(row("LISTS", me), V("SL"))
    send_all("ali%d" % me, "lli", row("LISTS", me))

    def offsets(q):
        ts(row("OFF", q), row("LISTS", q), 16.0 - 4096.0 * me, 4112.0, ADD, MIN)
    offsets(me)
    ts(V("w0"), V("PR"), 2048 * me, None, ADD)
    ts(V("w1"), V("w0"), 7, None, SHR)
    ts(V("w2"), V("w0"), 127, None, AND)
    vcopy(C("PT", 512 * me, 512 * me + 256), V("w1"))
    vcopy(C("PT", 512 * me + 256, 512 * me + 512), V("w2"))
    send_all("apt", "lpt", row("PT", me, 512))
    iota(V("QC"), [[0, 8], [1, 16]], 0)
    iota(V("TC16"), [[0, 16]], 1)
    iota(V("T16"), [[0, 128]], 16)
    for r in others:
        expect("ali%d" % r, NB, [row("LISTS", r)])
    expect("apt", NB * (nrank - 1), [row("PT", r, 512) for r in others])
    ts(V("P16I"), V("PCI"), 15, None, AND)
    vcopy(V("P16"), V("P16I"))
    ts(V("w3"), V("N16"), V("P16"), None, ADD)
    ts(V("w4"), V("w3"), 127, None, AND)
    vcopy(C("IDT", 1024, 1280), V("w4"))
    ts(V("w4"), V("w3"), 7, None, SHR)
    vcopy(row("IDT", 0, 256), V("w4"))
    order = [far, off[1 - me % 2], on[0]]
    for i, q in enumerate(order):
        offsets(q)
        vgather(row("REP", 2 * i, 1024), V("XW"), row("OFF", 2 * q, 64))
        sgather(row("REP", 2 * i + 1, 1024), V("XW"), row("OFF", 2 * q + 1, 64))
        send(q, "arep%d" % me, "lrep", blk("ALLT0", me), row("REP", i, 2048), e_on if q in on else e_off)
    for r in others:
        expect("arep%d" % r, NB, [blk("ALLT0", r)])
    vgather(row("ALLT0", 2 * me, 1024), V("XW"), row("OFF", 2 * me, 64))
    sgather(row("ALLT0", 2 * me + 1, 1024), V("XW"), row("OFF", 2 * me + 1, 64))
    iota(V("TC"), [[0, 8], [1, 128]], -1)
    iota(V("QC2"), [[0, 8], [1, 16]], 0, base=16)
    iota(V("TDI"), [[-1, 128]], 0, base=128)
    iota(V("CE"), [[0, 1]], 16)
    fill(V("EQ"), 1.0 / 16)
    afs(V("E16"), V("EQ"), [[-1, 128], [0, 16]], EQU, 0, 1)
    fill(C("PWIN", 6144, 12288), 0.0)
    for o in range(1, nrank):
        scopy(row("IDT", o, 256), row("IDT", 0, 256), bias=32.0 * o)
    scopy(C("PWIN", 12288, 16384), C("PWIN", 0, 4096))

    for o in range(nrank):
        for c in range(4):
            src = row("IDT", o if c == 0 else 4, 256) if c < 2 else row("PT", 2 * o + c - 2, 256)
            dma("y", "dpw%d" % (c // 2), C("PWIN", 4096 * o, 4096 * o + 4096, ps=slice(c, 128, 16), tag=c), src)
    for i in range(8):
        ts(row("BE", i), V("ONE"), C("B8", i, i + 1), 128.0, MUL, MUL)
    ts(V("NBE"), V("BE"), -1.0, None, MUL)
    ts(V("B8N"), V("B8"), -128.0, None, MUL)
    ts(V("B8P"), V("B8"), 128.0, None, MUL)
    fill(V("GS"), 0.0)
    for i in range(8):
        fill(C("GS", 144 * i, 144 * i + 16), 1.0)
    ts(V("q0"), V("SL"), 4, None, SHR)
    ts(V("q1"), V("SL"), 15, None, AND)
    ts(V("q2"), V("SL"), 12, None, SHR)
    ts(V("q1"), V("q1"), 256, None, MUL)
    ts(V("q2"), V("q2"), 3840, None, MUL)
    tt(V("q0"), V("q0"), V("q1"), ADD)
    tt(V("q0"), V("q0"), V("q2"), ADD)
    vcopy(V("ILST"), V("q0"))
    for i in range(8):
        ts(row("BXP", i, 16), C("ONE", 0, 16), C("B8", i, i + 1), 32.0, MUL, MUL)
    ts(V("BXN"), V("BXP"), -1.0, None, MUL)
    ts(V("BP"), V("B8"), 1024.0, None, MUL)
    ts(V("BN"), V("B8"), -1024.0, None, MUL)
    ts(V("TCN"), V("TC16"), -0.5, None, MUL)
    ts(V("TC16"), V("TC16"), 0.5, None, MUL)
    ts(V("TD"), V("TDI"), 0.125, None, MUL)
    ts(V("TDN"), V("TDI"), -0.125, None, MUL)

    banks = ("PS3", "PS4", "PS6", "PS7")
    mychip = sorted(on + [me])
    for n, r in enumerate([me] + on + sorted(off, key=lambda r: mychip[r % 2] != me)):
        for i, b in enumerate(banks):
            mm(V(b), V("IB"), row("ALLT0", 4 * r + i, 512), n == 0, n == 3)
    for i, b in enumerate(banks):
        if i % 2 == 0:
            ts(row("POOL", i, 512), V(b), -128.0, None, ADD)
        else:
            scopy(row("POOL", i, 512), V(b), bias=-128.0)

    def ranks_open():
        for h in (0, 1):
            mm(V("PS%d" % h), V("IB"), row("TC", h, 512), True, False)

    inf = ["INF0", "INF1", "INF2", "INF3"]

    def info_done(k, nxt):
        for j in range(16):
            mm(C("PS4", j, 512, 16), C(inf[k], j, 2048, 16), V("SEL"), True, True)
        if nxt is not None:
            scopy(V("IDSO"), C("PS4", 0, 256))
            send(me ^ nxt, "aids%d" % k, "lids", row("IDSP", k, 256), V("IDSO"))
        if nxt is not None and k > 0:
            scopy(V("PAF"), C("PS4", 384, 512))
            mm(C("PS7", 0, 128), V("PAF"), V("IF"), True, True)
            vcopy(V("PAL"), C("PS7", 0, 128))
        scopy(V("IDO", slice(0, 8)), C("PS4", 256, 384))
        if nxt is not None:
            scopy(V("IDO", slice(8, 16)), C("PS4", 256, 384))

    def vgath(a, b, tab):
        sgather(C("REP", a, b), blk(tab, me), C("PREYL", a // 16, b // 16))

    def vsum(a, bank):
        mm(V(bank), V("IB"), C("V", a, a + 512), True, False)
        mm(V(bank), V("IB"), C("REP", a, a + 512), False, True)

    def vround(a, bank):
        scopy(C("V", a, a + 512), V(bank), scale=0.5, bias=768.25)

    def vdve(a, b, tab):
        ttg(C("VS", a, b), blk(tab, me), C("PREYL", a // 16, b // 16), C("V", a, b), ADD)
        ts(C("VT", a, b), C("VS", a, b), 0.5, 768.25, MUL, ADD)
        ts(C("YXO", a, b), C("VT", a, b), -1408.0, None, ADD)

    bits = {1: 5, 2: 4, 4: 3, 8: 2}

    def half(name, s, sv, k=None, kv=None):
        ix = [ALL] * 6
        ix[bits[s]] = sv
        if k is not None:
            ix[bits[k]] = kv
        return V(name, *ix[1:])

    def stage(src, dst, s, k=None, desc=False):
        for kv in ((0, 1) if k else (None,)):
            lo, hi = half(src, s, 0, k, kv), half(src, s, 1, k, kv)
            if dst in ("E2O", "SI"):
                dl, dh = C(dst, 0, 128, 2), C(dst, 1, 128, 2)
            else:
                dl, dh = half(dst, s, 0, k, kv), half(dst, s, 1, k, kv)
            if desc != (kv == 1):
                dl, dh = dh, dl
            tt(dl, lo, hi, MIN)
            tt(dh, lo, hi, MAX)

    def merge(src, other, last, desc=False):
        stage(src, other, 8, None, desc)
        stage(other, src, 4, None, desc)
        stage(src, other, 2, None, desc)
        stage(other, last, 1, None, desc)

    for k, d in enumerate(DS):
        p = me ^ d
        isA = me < p
        npart = ecount(p)
        expect("aids%d" % k, npart, [row("IDSP", k, 256)])
        expect("ainf%d" % k, npart, [C(inf[k], 2048, 4096)])
        expect("ast%d" % k, npart, [C("POOL", 2048, 4096)])
        src, o16 = ("POOL", 0.0) if k == 0 else ("V16", 24576.0)
        for h in (0, 1):
            for j in range(16):
                mm(row("PS2", h, 64), V("IB"), C(src, 1024 * h + j, 1024 * h + 1024, 16), j == 0, j == 15)
        if k == 0:
            ranks_open()
            sgather(C("INF0", 0, 2048), V("PWIN"), V("ILST"))
        C16 = V("C16")
        ts(C16, C("PS2", 0, 128), -o16, None, ADD)
        mm(C("PS6", 384, 392), C16, V("B8N"), True, True)
        for gg in range(8):
            mm(row("PS%d" % (gg // 4), gg % 4), row("NBE", gg), C16, False, gg % 4 == 3)
        mm(C("PS7", 0, 128), C16, V("IB"), True, True)
        if k == 0:
            for c, (e, w) in enumerate(((0.0, 128.0), (1.0, 1.0), (2.0, 128.0), (3.0, 1.0))):
                ts(C("WC", c, c + 1), V("P16"), e, w, EQU, MUL)
            tt(C("WC", 4, 5), C("WC", 0, 1), C("WC", 1, 2), ADD)
            tt(C("WC", 5, 6), C("WC", 2, 3), C("WC", 3, 4), ADD)
            for c, w in enumerate((0, 1, 4, 5)):
                ts(row("SEL", c, 8), V("B8"), C("WC", w, w + 1), None, MUL)
        for gg in range(8):
            ts(row("G", gg), row("PS%d" % (gg // 4), gg % 4), C("PS6", 384 + gg, 385 + gg), None, GT)
        vcopy(C("E1O", 0, 128), C("PS7", 0, 128))
        for gg in range(8):
            mm(C("PS2", 128, 256), row("GS", gg), row("G", gg), gg == 0, gg == 7)
        ts(C("E1O", 128, 256), C("PS2", 128, 256), 1.0 / 2048, None, MUL)
        send(p, "ae1%d" % k, "le1", row("E1P", k, 256), V("E1O"))
        if k == 0:
            ts(V("IBP"), V("IB"), 2 * BIG, None, MUL)
            ts(V("IBN"), V("IB"), -2 * BIG, None, MUL)
            fill(V("NH"), -0.5)
            info_done(0, d)
        for i, b in enumerate(("PS5", "PS6", "PS7", "PS4")):
            mm(V(b), C("E1O", 0, 128), row("E16", i, 512), True, True)
            tt(row("Y1", i, 512), V(b), row("POOL", i, 512), MAX)
        for h in (0, 1):
            mm(V("PS%d" % h), V("ONE"), row("G", h, 512), True, True)
        send(p, "ast%d" % k, "lst", C("POOL", 2048, 4096), C("POOL", 0, 2048))
        send(p, "ainf%d" % k, "linf", C(inf[k], 2048, 4096), C(inf[k], 0, 2048))
        expect("ae1%d" % k, npart, [row("E1P", k, 256)])
        scopy(V("IDX", slice(0, 16), slice(0, 16)), row("IDSP", k, 256), scale=1.0 / 32)
        scopy(V("IDX", slice(16, 32), slice(8, 24)), row("IDSP", k, 256), scale=1.0 / 32)
        scopy(V("IDX", slice(0, 16), slice(16, 24)), V("IDX", slice(0, 16), slice(0, 8)))
        scopy(V("IDX", slice(16, 32), slice(0, 8)), V("IDX", slice(0, 16), slice(8, 16)))
        KEY = C("PS3", 0, 128)
        mm(KEY, V("IB"), V("QC" if isA else "QC2"), True, False)
        mm(KEY, C16, V("BXN" if isA else "BXP"), False, False)
        mm(C("PS6", 392, 400), row("E1P", 2 * k + 1), V("B8P"), True, True)
        for gg in range(8):
            ts(row("MA", gg), row("PS%d" % (gg // 4), gg % 4), C("PS6", 392 + gg, 393 + gg), 32.0, EQU, MUL)
        for j in range(16):
            mm(C("PS3", j, 128, 16), C("Y1", j, 2048, 16), V("BP" if isA else "BN"), False, False)
        for gg in range(8):
            mm(C("PS2", 256 + 16 * gg, 272 + 16 * gg), row("MA", gg), row("E1P", 16 * k + gg, 16), True, True)
        ts(V("CSM"), C("PS2", 256, 384), 1.0 / 32, None, MUL)
        Y2B = ("PS0", "PS1", "PS4", "PS7")
        for b in range(4):
            mm(V(Y2B[b]), V("CSM"), row("E16", b, 512), True, True)
        mm(C("PS6", 0, 128), V("CSM"), V("IB"), True, True)
        scopy(V("CBT"), C("PS6", 0, 128))
        scopy(V("MAF"), V("MA"), scale=1.0 / 32)
        for gg in range(8):
            for c in (0, 1):
                mm(V("PS5", slice(gg, 16, 8), slice(0, 24)), row("MA", gg), V("IDX", slice(8 * c + gg, 32, 16), slice(0, 24)),
                   c == 0, c == 1)
        for b in range(4):
            tt(row("Y2", b, 512), V(Y2B[b]), row("POOL", b, 512), MAX)
        IW, KC = (V("IBN"), "QC") if isA else (V("IBP"), "QC2")
        CM = C("PS6", 384, 512)
        mm(KEY, V("CBT"), V("BXP" if isA else "BXN"), False, False)
        mm(CM, V("IB"), V(KC), True, False)
        mm(CM, IW, V("NH"), False, False)
        for r in range(8):
            tt(row("EQ", r, 256), V("PS5", ALL, slice(r, r + 16)), V("IDO"), EQU)
            if r == 0:
                for j in range(16):
                    mm(C("PS3", j, 128, 16), C("Y2", j, 2048, 16), V("BN" if isA else "BP"), False, j == 15)
            for h in (0, 1):
                mm(CM, IW, row("EQ", 2 * r + h), False, r == 7 and h == 1)
            if r == 6:
                vcopy(V("K1"), KEY)
        tt(V("SRA"), V("K1"), CM, MIN if isA else MAX)
        if k == 0:
            scopy(V("V"), C("XW", 16, 4112), bias=1408.0)
            vcopy(V("IF"), V("IB"))
        else:
            for i, b in ((0, "PS4"), (1, "PS7"), (2, "PS0"), (3, "PS1"), (4, "PS3")):
                vsum(512 * i, b)
                vround(512 * i, b)
        desc = not isA
        stage("SRA", "SRB", 1, 2, desc)
        stage("SRB", "SRA", 2, 4, desc)
        stage("SRA", "SRB", 1, 4, desc)
        stage("SRB", "SRA", 4, 8, desc)
        stage("SRA", "SRB", 2, 8, desc)
        stage("SRB", "SRA", 1, 8, desc)
        merge("SRA", "SRB", "E2O", desc)
        send(p, "ae2%d" % k, "le2", row("E2P", k), V("E2O"))
        expect("ae2%d" % k, npart, [row("E2P", k)])
        if k == 0:
            vcopy(V("PREYL"), V("PR"))
        DIF = C("PS6", 128, 256)
        mm(DIF, V("TD" if isA else "TDN"), V("ONE"), True, False)
        for gg in range(8):
            mm(row("PS6", 8 + gg, 16), row("MA", gg), V("TC16" if isA else "TCN"), False, gg == 7)
        adj = V("T16")
        if not isA:
            adj = V("ADJ")
            ts(adj, DIF, -1.0, V("CE"), MUL, ADD)
        mm(C("PS2", 384, 512), adj, V("IB"), True, False)
        if isA:
            ts(V("SRB"), V("E2O"), -3000000.0, 2 * BIG, LT, MUL)
            tt(V("SRM"), V("E2O"), V("SRB"), ADD)
            merge("SRM", "SRB", "SRM")
            ts(V("SRB"), V("SRM"), 3000000.0, -2 * BIG, LT, MUL)
            tt(V("AMX"), V("SRM"), V("SRB"), ADD)
        for gg in range(8):
            mm(row("PS7", 8 + gg, 16), row("MAF", gg), row("E2P", 8 * k + gg, 16), True, True)
        if k == 2:
            for i, b in ((5, "PS0"), (6, "PS1")):
                vsum(512 * i, b)
                vround(512 * i, b)
        if isA:
            tt(V("SRA"), V("SRM"), C("PS7", 128, 256), MIN)
            merge("SRA", "SRB", "SRA")
            tt(V("SI"), V("SRA"), V("AMX"), MAX)
        else:
            tt(V("SRA"), V("E2O"), C("PS7", 128, 256), MAX)
            merge("SRA", "SRB", "SI")
        ts(V("BB"), V("SI"), 4, 1, SHR, AND)
        ts(V("QA"), V("SI"), 15, None, AND)
        tt(V("M1"), V("BB"), DIF, MUL)
        vcopy(V("QAB"), V("QA"))
        mm(C("PS2", 384, 512), V("M1"), V("IB"), False, False)
        mm(C("PS2", 384, 512), V("QAB"), V("IB"), False, True)
        vcopy(V("LST"), C("PS2", 384, 512))
        tab = "ALLT0" if k == 1 else "ALLT1"
        m0 = 2048 * me
        if k == 2:
            vgather(C(tab, m0, m0 + 1024), V("POOL"), C("LST", 0, 64))
            sgather(C(tab, m0 + 1024, m0 + 2048), V("POOL"), C("LST", 64, 128))
        else:
            for h in (0, 1):
                a = m0 + 1024 * h
                vgather(C(tab, a, a + 512), V("POOL"), C("LST", 64 * h, 64 * h + 32))
                sgather(C(tab, a + 512, a + 1024), V("POOL"), C("LST", 64 * h + 32, 64 * h + 64))
                send_parts([("ad3%d%d" % (k, h), [far], e_off), ("ae3%d" % k, on, e_on)], "le3", C(tab, a, a + 1024))
            piece = [C(tab, 2048 * far + 1024 * h, 2048 * far + 1024 * h + 1024) for h in (0, 1)]
            for h in (0, 1):
                expect("ad3%d%d" % (k, h), NB, [piece[h]])
            for h in (0, 1):
                send(on[0], "ae3%d" % k, "le3", piece[h], piece[h], e_hand[h])
            expect("ae3%d" % k, 2 * len(e_on) + len(e_hand[0]) + len(e_hand[1]), [blk(tab, r) for r in others if r != far])
        if k < 2:
            vcopy(C("V16", 0, 1024), C(tab, m0, m0 + 1024))
            sgather(C(inf[k + 1], 0, 2048), V(inf[k]), V("LST"))
            late = ((5, "PS0"), (6, "PS1"), (7, "PS3")) if k > 0 else ()
            for i, b in late:
                vsum(512 * i, b)
            info_done(k + 1, DS[k + 1])
            for i, b in late:
                vround(512 * i, b)
            ranks_open()
            ttg(V("SU"), V(tab), C("PAL", 0, 64), C("V16", 0, 1024), ADD)
            sgather(C("REP", 4096, 5120), V(tab), C("PAL", 64, 128))
            for h in (0, 1):
                mm(V("PS%d" % (6 + h)), V("IB"), C(tab, m0 + 1024 + 512 * h, m0 + 1536 + 512 * h), True, False)
            for h in (0, 1):
                mm(V("PS%d" % (6 + h)), V("IB"), row("REP", 8 + h, 512), False, True)
            ts(C("V16", 0, 1024), V("SU"), 0.5, 1536.25, MUL, ADD)
            ts(row("V16", 2, 512), V("PS6"), 0.5, 1536.25, MUL, ADD)
            scopy(row("V16", 3, 512), V("PS7"), scale=0.5, bias=1536.25)
            for a in (0, 1024, 2048, 3072):
                vgath(a, a + 1024, tab)
            ts(C("POOL", 0, 2048), V("V16"), -1536.0, None, ADD)
        else:
            def put(i, a, b):
                dma("y", "dyx%d" % i, None, C("YXO", a, b), ext_out=T.yx[:, a:b])

            def last(a):
                vround(a, "PS%d" % (a // 512 % 4))
                scopy(C("YXO", a, a + 512), C("V", a, a + 512), bias=-1408.0)
            vsum(3584, "PS4")
            vgath(2048, 3072, tab)
            vround(3584, "PS4")
            vgath(3072, 4096, tab)
            sgather(C("INF3", 1536, 2048), V(inf[k]), C("LST", 96, 128))
            for a in range(2048, 4096, 512):
                vsum(a, "PS%d" % (a // 512 % 4))
            vdve(0, 1024, tab)
            put(0, 0, 1024)
            vgather(C("INF3", 0, 1536), V(inf[k]), C("LST", 0, 96))
            last(2048)
            last(2560)
            put(1, 2048, 3072)
            vdve(1024, 1536, tab)
            put(2, 1024, 1536)
            info_done(3, None)
            mm(C("PS7", 0, 128), V("IDO", slice(0, 8)), V("IF"), True, True)
            scopy(V("YLO"), C("PS7", 0, 128))
            dma("y", "dyl", None, V("YLO"), ext_out=T.yl[:, :])
            vdve(1536, 2048, tab)
            put(3, 1536, 2048)
            last(3072)
            put(4, 3072, 3584)
            last(3584)
            put(5, 3584, 4096)
    for sem in sorted(tot):
        if know["g"].get(sem, 0) < tot[sem]:
            g.wait_ge(T.sem[sem], tot[sem])
